import numpy as np
import ml_dtypes


def mxq(x, axis, fmt="e4m3"):
    dtype, down = {"e4m3": (ml_dtypes.float8_e4m3fn, 7), "e5m2": (ml_dtypes.float8_e5m2, 14)}[fmt]
    v = np.moveaxis(np.asarray(x, np.float32).astype(ml_dtypes.bfloat16).astype(np.float64), axis, -1)
    blocks = v.reshape(v.shape[:-1] + (-1, 32))
    amax = np.abs(blocks).max(-1, keepdims=True)
    byte = np.maximum(np.where(amax > 0, np.frexp(amax)[1] - 1 + 127, 0) - down, 1)
    scale = np.exp2(byte - 127.0)
    codes = (blocks / scale).astype(np.float32).astype(dtype).astype(np.float64)
    return np.moveaxis((codes * scale).reshape(v.shape), -1, axis)


WIDE = False


def mx_kscale(k):
    if not WIDE:
        return np.ones(k)
    levels = np.array([10, -10, 5, -5, 0])
    if k % 512:
        return np.exp2(np.random.permutation(np.resize(levels, k // 32))).repeat(32)
    a = np.empty((k // 512, 16))
    for p in range(k // 512):
        a[p, :8] = np.random.permutation(np.resize(levels, 8))
        for g in range(8):
            far = levels[np.abs(levels - a[p, g]) >= 10]
            a[p, g + 8] = far[np.random.randint(len(far))]
    return np.exp2(a.ravel()).repeat(32)


def f64(x):
    return np.asarray(x).astype(np.float64)


def striped(idx):
    return np.tile(idx.reshape(-1, 16).T, (8, 1)).astype(np.uint16)


def unstriped(offs):
    return offs[:16].T.reshape(-1).astype(np.int64)


E2M1 = np.array([0.0, 0.5, 1.0, 1.5, 2.0, 3.0, 4.0, 6.0, -0.0, -0.5, -1.0, -1.5, -2.0, -3.0, -4.0, -6.0])


def pack_weight(w, fmt):
    k, n = w.shape
    w = f64(np.asarray(w, np.float32).astype(ml_dtypes.bfloat16)).reshape(k // 32, 32, n)
    amax = np.abs(w).max(1)
    if fmt == "e4m3":
        byte = np.frexp(amax)[1] - 1 + 127 - 7
    else:
        mant, ex = np.frexp(amax / 6.0)
        byte = np.where(mant > 0.5, ex, ex - 1) + 127
    byte = np.clip(np.where(amax > 0, byte, 1), 1, 254)
    scaled = (w * np.exp2(127.0 - byte)[:, None, :]).reshape(k, n).astype(np.float32)
    by_word = np.ascontiguousarray(scaled.reshape(k // 512, 128, 4, n).transpose(0, 1, 3, 2))
    if fmt == "e4m3":
        words = by_word.astype(ml_dtypes.float8_e4m3fn).view(np.uint8)
    else:
        c = by_word.astype(ml_dtypes.float4_e2m1fn).view(np.uint8) & 0xF
        words = (c[..., 0::2] | (c[..., 1::2] << 4)).reshape(k // 512, 128, 2 * n)
    return np.ascontiguousarray(words), np.ascontiguousarray(byte.astype(np.uint8).reshape(k // 512, 16, n))


def unpack_weight(words, scales, fmt):
    g, _, n = scales.shape
    words = np.ascontiguousarray(words).reshape(g, 128, n, -1)
    if fmt == "e4m3":
        vals = words.view(ml_dtypes.float8_e4m3fn).astype(np.float64)
    else:
        nib = np.empty((g, 128, n, 4), np.uint8)
        nib[..., 0::2] = words & 0xF
        nib[..., 1::2] = words >> 4
        vals = E2M1[nib]
    vals = vals * np.repeat(np.exp2(scales.astype(np.float64) - 127.0), 8, axis=1)[..., None]
    return vals.transpose(0, 1, 3, 2).reshape(g * 512, n)


def relu2(v):
    return np.maximum(v, 0.0) ** 2


K, T, E, C, H, HS, N = 512, 512, 8, 128, 512, 512, 512


def by_expert(wq, xq):
    return np.concatenate([wq[e].T @ xq[:, e * C:(e + 1) * C] for e in range(E)], axis=1)


def setup_inputs():
    n = np.random.standard_normal
    s = mx_kscale(K)
    u = mx_kscale(H)
    v = mx_kscale(HS)
    first = np.random.permutation(np.repeat(np.arange(E), T // E))
    second = (first + 1 + np.random.permutation(np.repeat(np.arange(E - 1), -(-T // (E - 1)))[:T])) % E
    while np.bincount(second, minlength=E).max() != T // E:
        load = np.bincount(second, minlength=E); hi, lo = int(load.argmax()), int(load.argmin())
        t = np.flatnonzero((second == hi) & (first != lo))[0]; second[t] = lo
    slot_token = np.empty(E * C, np.int64); pos = np.empty((2, T), np.int64); fill = np.zeros(E, np.int64)
    place = np.stack([np.random.permutation(C) for _ in range(E)])
    for r, deal in enumerate((first, second)):
        for t in np.random.permutation(T):
            e = deal[t]; j = e * C + place[e, fill[e]]; fill[e] += 1; slot_token[j] = t; pos[r, t] = j
    g = np.random.uniform(0.2, 0.8, T)
    x = pack_weight(n((K, T)) * s[:, None], "e4m3")
    w1 = [pack_weight(m, "e2m1") for m in n((E, K, H)) / np.sqrt(K) / s[None, :, None] * u]
    w2 = [pack_weight(m, "e2m1") for m in n((E, H, N)) / np.sqrt(H) / u[None, :, None] ** 2]
    w1s = pack_weight(n((K, HS)) / np.sqrt(K) / s[:, None] * v, "e4m3")
    w2s = pack_weight(n((HS, N)) / np.sqrt(HS) / v[:, None] ** 2, "e4m3")
    return {
        "x_words": x[0],
        "x_scales": x[1],
        "w1_words": np.stack([m[0] for m in w1]),
        "w1_scales": np.stack([m[1] for m in w1]),
        "w2_words": np.stack([m[0] for m in w2]),
        "w2_scales": np.stack([m[1] for m in w2]),
        "w1s_words": w1s[0],
        "w1s_scales": w1s[1],
        "w2s_words": w2s[0],
        "w2s_scales": w2s[1],
        "gate": np.stack([np.tile(g, (128, 1)), np.tile(1.0 - g, (128, 1))]).astype(np.float32),
        "offs": striped(slot_token),
        "pos1": striped(pos[0]),
        "pos2": striped(pos[1]),
    }


def reference(x_words, x_scales, w1_words, w1_scales, w2_words, w2_scales, w1s_words, w1s_scales, w2s_words, w2s_scales, gate, offs, pos1, pos2):
    w1 = np.stack([unpack_weight(w1_words[e], w1_scales[e], "e2m1") for e in range(E)])
    w2 = np.stack([unpack_weight(w2_words[e], w2_scales[e], "e2m1") for e in range(E)])
    w1s = unpack_weight(w1s_words, w1s_scales, "e4m3")
    w2s = unpack_weight(w2s_words, w2s_scales, "e4m3")
    idx = unstriped(offs)
    x = unpack_weight(x_words, x_scales, "e4m3")
    hs = relu2(w1s.T @ x)
    ys = w2s.T @ mxq(hs, 0, "e4m3")
    h = relu2(by_expert(w1, x[:, idx]))
    y = by_expert(w2, mxq(h, 0, "e4m3"))
    c = sum(f64(gate[r, :1]) * y[:, unstriped(p)] for r, p in enumerate((pos1, pos2)))
    return ys + c

@@ -1,0 +1,260 @@
+from contextlib import ExitStack
+
+import concourse.mybir as mybir
+from concourse.masks import make_identity
+
+K, T, E, C, H, HS, N = 512, 512, 8, 128, 512, 512, 512
+S = E * C
+FLOPS = 2 * K * H * S + 2 * H * N * S + 2 * K * HS * T + 2 * HS * N * T
+
+F32 = mybir.dt.float32
+BF16 = mybir.dt.bfloat16
+I32 = mybir.dt.int32
+U32 = mybir.dt.uint32
+U16 = mybir.dt.uint16
+U8 = mybir.dt.uint8
+FP8X4 = mybir.dt.float8_e4m3fn_x4
+FP4X4 = mybir.dt.float4_e2m1fn_x4
+ACT = mybir.ActivationFunctionType
+ALU = mybir.AluOpType
+
+P = 128
+NT = N // P
+
+
+def tile_moe_shf_mlp_relu2_kernel(
+    tc, x_words, x_scales, w1_words, w1_scales, w2_words, w2_scales,
+    w1s_words, w1s_scales, w2s_words, w2s_scales, gate, offs, pos1, pos2, out,
+):
+    nc = tc.nc
+    with ExitStack() as ctx:
+        keep = ctx.enter_context(tc.tile_pool(name="keep", bufs=1))
+        ring = ctx.enter_context(tc.tile_pool(name="ring", bufs=3))
+        psum = ctx.enter_context(tc.psum_pool(name="psum", bufs=1))
+
+        def held(name, shape, dtype):
+            return keep.tile(shape, dtype, name=name, align_bytes=64)
+
+        def bank(b, shape):
+            return psum.tile(shape, F32, name="bank%d" % b)
+
+        offs_t = keep.tile([P, S // 16], U16, name="offs_t")
+        pos_t = [keep.tile([P, T // 16], U16, name="pos_t%d" % r) for r in range(2)]
+        xw = held("xw", [P, T], I32)
+        xs = held("xs", [P, T], U8)
+        xgw = [held("xgw%d" % g, [P, 2 * C], U32) for g in range(4)]
+        xgs = [held("xgs%d" % g, [P, 2 * C], U8) for g in range(4)]
+        w1w = [held("w1w%d" % g, [P, 2, 2 * H], U8) for g in range(4)]
+        w1c = held("w1c", [P, E, H], U8)
+        w2w = [held("w2w%d" % g, [P, 4, 2 * N], U8) for g in range(2)]
+        w2c = held("w2c", [P, E, N], U8)
+        w1sw = held("w1sw", [P, HS], I32)
+        w1sc = held("w1sc", [P, HS], U8)
+        w2sw = held("w2sw", [P, N], I32)
+        w2sc = held("w2sc", [P, N], U8)
+        gate_t = held("gate_t", [P, 2, T], F32)
+        ident = held("ident", [P, P], F32)
+        widths = [2 * C] * 4 + [T]
+        hb = [held("hb%d" % g, [P, w, 4], BF16) for g, w in enumerate(widths)]
+        hw = [held("hw%d" % g, [P, w], U32) for g, w in enumerate(widths)]
+        hc = [held("hc%d" % g, [P, w], U8) for g, w in enumerate(widths)]
+        y = [held("y%d" % j, [P, S], F32) for j in range(NT)]
+        warm = held("warm", [P, 8], F32)
+
+        def zero(plane):
+            nc.vector.memset(plane.bitcast(I32), 0)
+
+        def load_words(dst, src):
+            nc.sync.dma_start(dst[:], src[0].rearrange("p t d -> p (t d)").bitcast(I32))
+
+        def load_plane(dst, src):
+            for q in range(4):
+                rows = src[0, 4 * q : 4 * q + 4, :].bitcast(I32)
+                nc.sync.dma_start(
+                    dst[32 * q : 32 * (q + 1), :].bitcast(I32), rows.unsqueeze(0).to_broadcast([8, 4, rows.shape[1]])
+                )
+
+        def load_expert_planes(dst, src, queue):
+            for q in range(4):
+                queue.dma_start(
+                    dst[32 * q : 32 * q + 4, :, :].bitcast(I32),
+                    src[:, 0, 4 * q : 4 * q + 4, :].rearrange("e b i -> b e i").bitcast(I32),
+                )
+
+        def load_expert_words(dst, src, e0, e1):
+            nc.sync.dma_start(
+                dst[:].bitcast(I32), src[e0:e1, 0].rearrange("e p c -> p e c").bitcast(I32)
+            )
+
+        zero(w2c[:].rearrange("p e i -> p (e i)"))
+        zero(w1c[:].rearrange("p e i -> p (e i)"))
+        nc.gpsimd.memset(warm[:], 0.0)
+        nc.scalar.activation(warm[:, 4:5], warm[:, 0:1], ACT.Square)
+        make_identity(nc, ident[:])
+
+        load_expert_planes(w2c, w2_scales, nc.gpsimd)
+        load_plane(xs, x_scales)
+        load_words(xw, x_words)
+        nc.sync.dma_start(offs_t[:], offs)
+        load_expert_words(w1w[0], w1_words, 0, 2)
+        load_expert_planes(w1c, w1_scales, nc.sync)
+        for g in range(1, 4):
+            load_expert_words(w1w[g], w1_words, 2 * g, 2 * g + 2)
+        load_plane(w1sc, w1s_scales)
+        load_words(w1sw, w1s_words)
+        load_expert_words(w2w[0], w2_words, 0, 4)
+        load_expert_words(w2w[1], w2_words, 4, 8)
+        nc.sync.dma_start(pos_t[0][:], pos1)
+        nc.sync.dma_start(pos_t[1][:], pos2)
+        nc.sync.dma_start(gate_t[:], gate.rearrange("r p t -> p r t"))
+        load_plane(w2sc, w2s_scales)
+        load_words(w2sw, w2s_words)
+
+        def gather_tokens(pair):
+            lst = offs_t[:, 16 * pair : 16 * (pair + 1)]
+            nc.vector.tensor_copy(xgw[pair][:], xw[:].bitcast(U32).indirect(lst))
+            nc.vector.tensor_copy(xgs[pair][:], xs[:].indirect(lst))
+
+        pre = {}
+        rect = {}
+        turned = {}
+
+        def layer1(u):
+            pre[u] = bank(u % 3, [P, H])
+            if u < E:
+                cols = slice(C * (u % 2), C * (u % 2 + 1))
+                nc.tensor.matmul_mx(
+                    out=pre[u][:], lhsT=xgw[u // 2][:, cols].bitcast(FP8X4), lhsT_scale=xgs[u // 2][:, cols],
+                    rhs=w1w[u // 2][:, u % 2, :].bitcast(FP4X4), rhs_scale=w1c[:, u, :], start=True, stop=True,
+                )
+            else:
+                cols = slice(C * (u - E), C * (u - E + 1))
+                nc.tensor.matmul_mx(
+                    out=pre[u][:], lhsT=xw[:, cols].bitcast(FP8X4), lhsT_scale=xs[:, cols],
+                    rhs=w1sw[:].bitcast(FP8X4), rhs_scale=w1sc[:], start=True, stop=True,
+                )
+
+        def rectify(u, on_vector):
+            rect[u] = ring.tile([P, 4, P], F32, name="rect")
+            src = pre[u][:].rearrange("s (m t) -> s t m", t=4)
+            if on_vector:
+                nc.vector.tensor_scalar_max(rect[u][:], src, 0.0)
+            else:
+                nc.scalar.activation(rect[u][:], src, ACT.Relu)
+
+        def turn(u):
+            turned[u] = bank(3 + u % 3, [P, 4, P])
+            for t in range(4):
+                nc.tensor.transpose(turned[u][:, t, :], rect[u][:, t, :], ident[:])
+
+        def square(u):
+            g, k = (u // 2, u % 2) if u < E else (4, u - E)
+            nc.scalar.activation(hb[g][:, C * k : C * (k + 1), :], turned[u][:].rearrange("p t s -> p s t"), ACT.Square)
+
+        def quantise(g):
+            nc.vector.quantize_mx(
+                out=hw[g][:].bitcast(FP8X4), scales=hc[g][:], in_=hb[g][:].rearrange("p s t -> p (s t)"),
+            )
+
+        def layer2(acc, e, j):
+            cols = slice(C * (e % 2), C * (e % 2 + 1))
+            nc.tensor.matmul_mx(
+                out=acc[:, C * (e % 4) : C * (e % 4 + 1)],
+                lhsT=w2w[e // 4][:, e % 4, 2 * P * j : 2 * P * (j + 1)].bitcast(FP4X4), lhsT_scale=w2c[:, e, P * j : P * (j + 1)],
+                rhs=hw[e // 2][:, cols].bitcast(FP8X4), rhs_scale=hc[e // 2][:, cols], start=True, stop=True,
+            )
+
+        gather_tokens(0)
+        gather_tokens(1)
+        layer1(0)
+        layer1(1)
+        rectify(0, False)
+        rectify(1, False)
+        y0_acc = [bank(6, [P, 4 * C]), bank(7, [P, 4 * C])]
+        for pair in range(4):
+            a, b = 2 * pair, 2 * pair + 1
+            if pair + 2 < 4:
+                gather_tokens(pair + 2)
+            turn(a)
+            turn(b)
+            layer1(a + 2)
+            layer1(b + 2)
+            square(a)
+            rectify(a + 2, pair >= 2)
+            square(b)
+            rectify(b + 2, True)
+            quantise(pair)
+            layer2(y0_acc[pair // 2], a, 0)
+            layer2(y0_acc[pair // 2], b, 0)
+            if pair == 1:
+                nc.scalar.copy(y[0][:, 0 : 4 * C], y0_acc[0][:])
+            if pair >= 2:
+                nc.scalar.copy(y[0][:, C * a : C * (b + 1)], y0_acc[1][:, C * (a - 4) : C * (b - 3)])
+
+        def routed_rows(j, banks):
+            for half in range(2):
+                acc = bank(banks[half], [P, 4 * C])
+                for e in range(4 * half, 4 * half + 4):
+                    layer2(acc, e, j)
+                nc.scalar.copy(y[j][:, 4 * C * half : 4 * C * (half + 1)], acc[:])
+
+        picked = {}
+
+        def pick(j, r, t0=0, t1=T):
+            picked[j, r, t0] = held("picked%d_%d_%d" % (j, r, t0), [P, t1 - t0], F32)
+            nc.vector.tensor_tensor(
+                picked[j, r, t0][:], y[j][:].indirect(pos_t[r][:, t0 // 16 : t1 // 16]), gate_t[:, r, t0:t1], ALU.mult
+            )
+
+        turn(8)
+        turn(9)
+        layer1(10)
+        layer1(11)
+        rectify(10, True)
+        rectify(11, True)
+        pick(0, 0)
+        routed_rows(1, (6, 7))
+        pick(0, 1)
+        square(8)
+        square(9)
+        turn(10)
+        turn(11)
+        square(10)
+        square(11)
+        pick(1, 0)
+        quantise(4)
+        pick(1, 1)
+        ys = []
+        for j in range(NT):
+            ys.append(bank(j, [P, T]))
+            nc.tensor.matmul_mx(
+                out=ys[j][:], lhsT=w2sw[:, P * j : P * (j + 1)].bitcast(FP8X4), lhsT_scale=w2sc[:, P * j : P * (j + 1)],
+                rhs=hw[4][:].bitcast(FP8X4), rhs_scale=hc[4][:], start=True, stop=True,
+            )
+        routed_rows(2, (6, 7))
+        routed_rows(3, (4, 5))
+
+        part = [held("part%d" % j, [P, T], F32) for j in range(NT)]
+
+        def add_shared(j):
+            nc.vector.tensor_tensor(part[j][:], picked[j, 0, 0][:], ys[j][:], ALU.add)
+
+        def finish(j, t0=0, t1=T):
+            res = held("res%d_%d" % (j, t0), [P, t1 - t0], F32)
+            nc.vector.tensor_tensor(res[:], part[j][:, t0:t1], picked[j, 1, t0][:], ALU.add)
+            nc.sync.dma_start(out[P * j : P * (j + 1), t0:t1], res[:])
+
+        add_shared(0)
+        pick(2, 0)
+        finish(0)
+        add_shared(1)
+        pick(2, 1)
+        finish(1)
+        add_shared(2)
+        pick(3, 0)
+        finish(2)
+        add_shared(3)
+        pick(3, 1, 0, T // 2)
+        pick(3, 1, T // 2, T)
+        finish(3, 0, T // 2)
+        finish(3, T // 2, T)

@@ -29,7 +29,7 @@ def tile_moe_shf_mlp_relu2_kernel(
     nc = tc.nc
     with ExitStack() as ctx:
         keep = ctx.enter_context(tc.tile_pool(name="keep", bufs=1))
-        ring = ctx.enter_context(tc.tile_pool(name="ring", bufs=3))
+        ring = ctx.enter_context(tc.tile_pool(name="ring", bufs=5))
         psum = ctx.enter_context(tc.psum_pool(name="psum", bufs=1))
 
         def held(name, shape, dtype):
@@ -86,13 +86,12 @@ def tile_moe_shf_mlp_relu2_kernel(
                 dst[:].bitcast(I32), src[e0:e1, 0].rearrange("e p c -> p e c").bitcast(I32)
             )
 
-        zero(w2c[:].rearrange("p e i -> p (e i)"))
         zero(w1c[:].rearrange("p e i -> p (e i)"))
+        zero(w2c[:].rearrange("p e i -> p (e i)"))
         nc.gpsimd.memset(warm[:], 0.0)
         nc.scalar.activation(warm[:, 4:5], warm[:, 0:1], ACT.Square)
         make_identity(nc, ident[:])
 
-        load_expert_planes(w2c, w2_scales, nc.gpsimd)
         load_plane(xs, x_scales)
         load_words(xw, x_words)
         nc.sync.dma_start(offs_t[:], offs)
@@ -104,9 +103,10 @@ def tile_moe_shf_mlp_relu2_kernel(
         load_words(w1sw, w1s_words)
         load_expert_words(w2w[0], w2_words, 0, 4)
         load_expert_words(w2w[1], w2_words, 4, 8)
-        nc.sync.dma_start(pos_t[0][:], pos1)
-        nc.sync.dma_start(pos_t[1][:], pos2)
-        nc.sync.dma_start(gate_t[:], gate.rearrange("r p t -> p r t"))
+        load_expert_planes(w2c, w2_scales, nc.sync)
+        for r, pos in enumerate((pos1, pos2)):
+            nc.sync.dma_start(pos_t[r][:], pos)
+            nc.sync.dma_start(gate_t[:, r, :], gate[r])
         load_plane(w2sc, w2s_scales)
         load_words(w2sw, w2s_words)
 
@@ -143,7 +143,7 @@ def tile_moe_shf_mlp_relu2_kernel(
                 nc.scalar.activation(rect[u][:], src, ACT.Relu)
 
         def turn(u):
-            turned[u] = bank(3 + u % 3, [P, 4, P])
+            turned[u] = bank(3 + u % 3 if u < E else (5, 6, 7, 3)[u - E], [P, 4, P])
             for t in range(4):
                 nc.tensor.transpose(turned[u][:, t, :], rect[u][:, t, :], ident[:])
 
@@ -151,9 +151,10 @@ def tile_moe_shf_mlp_relu2_kernel(
             g, k = (u // 2, u % 2) if u < E else (4, u - E)
             nc.scalar.activation(hb[g][:, C * k : C * (k + 1), :], turned[u][:].rearrange("p t s -> p s t"), ACT.Square)
 
-        def quantise(g):
+        def quantise(g, c0=0, c1=None):
             nc.vector.quantize_mx(
-                out=hw[g][:].bitcast(FP8X4), scales=hc[g][:], in_=hb[g][:].rearrange("p s t -> p (s t)"),
+                out=hw[g][:, c0:c1].bitcast(FP8X4), scales=hc[g][:, c0:c1],
+                in_=hb[g][:, c0:c1, :].rearrange("p s t -> p (s t)"),
             )
 
         def layer2(acc, e, j):
@@ -164,32 +165,28 @@ def tile_moe_shf_mlp_relu2_kernel(
                 rhs=hw[e // 2][:, cols].bitcast(FP8X4), rhs_scale=hc[e // 2][:, cols], start=True, stop=True,
             )
 
-        gather_tokens(0)
-        gather_tokens(1)
-        layer1(0)
-        layer1(1)
-        rectify(0, False)
-        rectify(1, False)
-        y0_acc = [bank(6, [P, 4 * C]), bank(7, [P, 4 * C])]
         for pair in range(4):
-            a, b = 2 * pair, 2 * pair + 1
-            if pair + 2 < 4:
-                gather_tokens(pair + 2)
-            turn(a)
-            turn(b)
-            layer1(a + 2)
-            layer1(b + 2)
-            square(a)
-            rectify(a + 2, pair >= 2)
-            square(b)
-            rectify(b + 2, True)
-            quantise(pair)
-            layer2(y0_acc[pair // 2], a, 0)
-            layer2(y0_acc[pair // 2], b, 0)
-            if pair == 1:
-                nc.scalar.copy(y[0][:, 0 : 4 * C], y0_acc[0][:])
-            if pair >= 2:
-                nc.scalar.copy(y[0][:, C * a : C * (b + 1)], y0_acc[1][:, C * (a - 4) : C * (b - 3)])
+            gather_tokens(pair)
+        for u in range(3):
+            layer1(u)
+        for u in range(3):
+            rectify(u, False)
+        for u in range(E):
+            layer1(u + 3)
+            turn(u)
+            square(u)
+            if u >= 5:
+                quantise(u - 5)
+            if u == E - 1:
+                quantise(3, 0, C)
+                quantise(3, C, 2 * C)
+            rectify(u + 3, True)
+        y0_acc = [bank(6, [P, 4 * C]), bank(7, [P, 4 * C]), bank(3, [P, 4 * C])]
+        for e in range(E):
+            layer2(y0_acc[e // 4 + e // 7], e, 0)
+        nc.scalar.copy(y[0][:, 0 : 4 * C], y0_acc[0][:])
+        nc.vector.tensor_copy(y[0][:, 4 * C : 7 * C], y0_acc[1][:, 0 : 3 * C])
+        nc.scalar.copy(y[0][:, 7 * C : 8 * C], y0_acc[2][:, 3 * C : 4 * C])
 
         def routed_rows(j, banks):
             for half in range(2):
@@ -206,55 +203,76 @@ def tile_moe_shf_mlp_relu2_kernel(
                 picked[j, r, t0][:], y[j][:].indirect(pos_t[r][:, t0 // 16 : t1 // 16]), gate_t[:, r, t0:t1], ALU.mult
             )
 
-        turn(8)
-        turn(9)
-        layer1(10)
-        layer1(11)
-        rectify(10, True)
-        rectify(11, True)
-        pick(0, 0)
-        routed_rows(1, (6, 7))
-        pick(0, 1)
-        square(8)
-        square(9)
-        turn(10)
-        turn(11)
-        square(10)
-        square(11)
-        pick(1, 0)
-        quantise(4)
-        pick(1, 1)
-        ys = []
-        for j in range(NT):
-            ys.append(bank(j, [P, T]))
+        ys = {}
+
+        def shared_rows(j, b):
+            ys[j] = bank(b, [P, T])
             nc.tensor.matmul_mx(
                 out=ys[j][:], lhsT=w2sw[:, P * j : P * (j + 1)].bitcast(FP8X4), lhsT_scale=w2sc[:, P * j : P * (j + 1)],
                 rhs=hw[4][:].bitcast(FP8X4), rhs_scale=hc[4][:], start=True, stop=True,
             )
-        routed_rows(2, (6, 7))
-        routed_rows(3, (4, 5))
 
-        part = [held("part%d" % j, [P, T], F32) for j in range(NT)]
+        ys_sb = {}
+        summed = {}
 
-        def add_shared(j):
-            nc.vector.tensor_tensor(part[j][:], picked[j, 0, 0][:], ys[j][:], ALU.add)
+        def park_shared(j):
+            ys_sb[j] = held("ys_sb%d" % j, [P, T], F32)
+            nc.scalar.copy(ys_sb[j][:], ys[j][:])
 
-        def finish(j, t0=0, t1=T):
-            res = held("res%d_%d" % (j, t0), [P, t1 - t0], F32)
-            nc.vector.tensor_tensor(res[:], part[j][:, t0:t1], picked[j, 1, t0][:], ALU.add)
-            nc.sync.dma_start(out[P * j : P * (j + 1), t0:t1], res[:])
+        def sum_turned(j, b):
+            acc = bank(b, [P, 4, P])
+            terms = (picked[j, 0, 0], ys_sb[j], picked[j, 1, 0])
+            for tb in range(4):
+                for k, term in enumerate(terms):
+                    nc.tensor.matmul(
+                        acc[:, tb, :], term[:, P * tb : P * (tb + 1)], ident[:],
+                        start=(k == 0), stop=(k == len(terms) - 1), is_transpose=True,
+                    )
+            summed[j] = held("summed%d" % j, [P, 4, P], F32)
+            nc.scalar.copy(summed[j][:], acc[:])
 
-        add_shared(0)
+        def turn_back(j, b):
+            acc = bank(b, [P, 4, P])
+            for tb in range(4):
+                nc.tensor.transpose(acc[:, tb, :], summed[j][:, tb, :], ident[:])
+            res = held("res%d" % j, [P, T], F32)
+            nc.scalar.copy(res[:], acc[:].rearrange("p a b -> p (a b)"))
+            (nc.scalar if j < 2 else nc.sync).dma_start(out[P * j : P * (j + 1), :], res[:])
+
+        layer1(11)
+        rectify(11, True)
+        pick(0, 0)
+        pick(0, 1)
+        for u in range(8, 12):
+            turn(u)
+            square(u)
+        quantise(4)
+        routed_rows(1, (6, 7))
+        pick(1, 0)
+        pick(1, 1)
+        routed_rows(2, (3, 6))
+        for j in range(NT):
+            shared_rows(j, (0, 1, 2, 4)[j])
+        park_shared(0)
+        park_shared(1)
+        routed_rows(3, (7, 3))
         pick(2, 0)
-        finish(0)
-        add_shared(1)
+        sum_turned(0, 5)
         pick(2, 1)
-        finish(1)
-        add_shared(2)
+        sum_turned(1, 0)
+        park_shared(2)
+        turn_back(0, 1)
         pick(3, 0)
-        finish(2)
-        add_shared(3)
-        pick(3, 1, 0, T // 2)
-        pick(3, 1, T // 2, T)
-        finish(3, 0, T // 2)
-        finish(3, T // 2, T)
+        sum_turned(2, 2)
+        turn_back(1, 5)
+        turn_back(2, 6)
+
+        part = held("part", [P, T], F32)
+        halves = ((0, T // 2), (T // 2, T))
+        pick(3, 1, *halves[0])
+        nc.vector.tensor_tensor(part[:], picked[3, 0, 0][:], ys[3][:], ALU.add)
+        pick(3, 1, *halves[1])
+        for t0, t1 in halves:
+            res = held("res3_%d" % t0, [P, t1 - t0], F32)
+            nc.vector.tensor_tensor(res[:], part[:, t0:t1], picked[3, 1, t0][:], ALU.add)
+            nc.sync.dma_start(out[P * 3 : P * 4, t0:t1], res[:])

@@ -19,6 +19,7 @@ ACT = mybir.ActivationFunctionType
 ALU = mybir.AluOpType
 
 P = 128
+CFG = {"A":[6,1,2,3,6,5,0,2,5,0,1,2],"B":[4,7,1,3,4,6,7,4,5,0,7,3],"d":4,"V":[0,0,1,0,1,1,1,1,1,1,1,1],"lfirst":1,"y0":[6,7,3],"ye":[0,1,1],"y1":[4,4],"y2":[3,5],"y3":[5,3],"ys":[4,2,1,0],"z":[7,1,3],"o":[4,2,1],"rb":5,"h":384,"q":[5,6,7],"ord":["ys","k0","k1","k2","z0","y2","z1","y3","o0","p2","z2","p3","o1","o2"],"sh":10,"sh2":12,"n":3,"cut":512,"early":0,"ld":["s1","b","l0","l1","a","s2"]}
 NT = N // P
 
 
@@ -29,7 +30,7 @@ def tile_moe_shf_mlp_relu2_kernel(
     nc = tc.nc
     with ExitStack() as ctx:
         keep = ctx.enter_context(tc.tile_pool(name="keep", bufs=1))
-        ring = ctx.enter_context(tc.tile_pool(name="ring", bufs=5))
+        ring = ctx.enter_context(tc.tile_pool(name="ring", bufs=CFG["rb"]))
         psum = ctx.enter_context(tc.psum_pool(name="psum", bufs=1))
 
         def held(name, shape, dtype):
@@ -46,8 +47,9 @@ def tile_moe_shf_mlp_relu2_kernel(
         xgs = [held("xgs%d" % g, [P, 2 * C], U8) for g in range(4)]
         w1w = [held("w1w%d" % g, [P, 2, 2 * H], U8) for g in range(4)]
         w1c = held("w1c", [P, E, H], U8)
-        w2w = [held("w2w%d" % g, [P, 4, 2 * N], U8) for g in range(2)]
-        w2c = held("w2c", [P, E, N], U8)
+        CUT = CFG["cut"]
+        w2w = [held("w2w%d" % g, [P, E, 2 * w], U8) for g, w in enumerate((CUT, N - CUT)) if w]
+        w2c = [held("w2c%d" % g, [P, E, w], U8) for g, w in enumerate((CUT, N - CUT)) if w]
         w1sw = held("w1sw", [P, HS], I32)
         w1sc = held("w1sc", [P, HS], U8)
         w2sw = held("w2sw", [P, N], I32)
@@ -74,11 +76,11 @@ def tile_moe_shf_mlp_relu2_kernel(
                     dst[32 * q : 32 * (q + 1), :].bitcast(I32), rows.unsqueeze(0).to_broadcast([8, 4, rows.shape[1]])
                 )
 
-        def load_expert_planes(dst, src, queue):
+        def load_expert_planes(dst, src, c0, c1):
             for q in range(4):
-                queue.dma_start(
-                    dst[32 * q : 32 * q + 4, :, :].bitcast(I32),
-                    src[:, 0, 4 * q : 4 * q + 4, :].rearrange("e b i -> b e i").bitcast(I32),
+                nc.sync.dma_start(
+                    dst[q:P:32, :, :].bitcast(I32),
+                    src[:, 0, q:16:4, c0:c1].rearrange("e b i -> b e i").bitcast(I32),
                 )
 
         def load_expert_words(dst, src, e0, e1):
@@ -87,7 +89,8 @@ def tile_moe_shf_mlp_relu2_kernel(
             )
 
         zero(w1c[:].rearrange("p e i -> p (e i)"))
-        zero(w2c[:].rearrange("p e i -> p (e i)"))
+        for plane in w2c:
+            zero(plane[:].rearrange("p e i -> p (e i)"))
         nc.gpsimd.memset(warm[:], 0.0)
         nc.scalar.activation(warm[:, 4:5], warm[:, 0:1], ACT.Square)
         make_identity(nc, ident[:])
@@ -96,19 +99,28 @@ def tile_moe_shf_mlp_relu2_kernel(
         load_words(xw, x_words)
         nc.sync.dma_start(offs_t[:], offs)
         load_expert_words(w1w[0], w1_words, 0, 2)
-        load_expert_planes(w1c, w1_scales, nc.sync)
+        load_expert_planes(w1c, w1_scales, 0, H)
         for g in range(1, 4):
             load_expert_words(w1w[g], w1_words, 2 * g, 2 * g + 2)
-        load_plane(w1sc, w1s_scales)
-        load_words(w1sw, w1s_words)
-        load_expert_words(w2w[0], w2_words, 0, 4)
-        load_expert_words(w2w[1], w2_words, 4, 8)
-        load_expert_planes(w2c, w2_scales, nc.sync)
-        for r, pos in enumerate((pos1, pos2)):
-            nc.sync.dma_start(pos_t[r][:], pos)
+        def load_w2(c0, c1):
+            nc.sync.dma_start(
+                w2w[c0 > 0][:].bitcast(I32),
+                w2_words[:, 0, :, 2 * c0 : 2 * c1].rearrange("e p c -> p e c").bitcast(I32),
+            )
+            load_expert_planes(w2c[c0 > 0], w2_scales, c0, c1)
+
+        def load_list(r):
+            nc.sync.dma_start(pos_t[r][:], (pos1, pos2)[r])
             nc.sync.dma_start(gate_t[:, r, :], gate[r])
-        load_plane(w2sc, w2s_scales)
-        load_words(w2sw, w2s_words)
+
+        loads = {
+            "a": lambda: load_w2(0, CFG["cut"]), "b": lambda: load_w2(CFG["cut"], N) if CFG["cut"] < N else None,
+            "s1": lambda: [load_plane(w1sc, w1s_scales), load_words(w1sw, w1s_words)],
+            "s2": lambda: [load_plane(w2sc, w2s_scales), load_words(w2sw, w2s_words)],
+            "l0": lambda: load_list(0), "l1": lambda: load_list(1),
+        }
+        for name in CFG["ld"]:
+            loads[name]()
 
         def gather_tokens(pair):
             lst = offs_t[:, 16 * pair : 16 * (pair + 1)]
@@ -120,7 +132,7 @@ def tile_moe_shf_mlp_relu2_kernel(
         turned = {}
 
         def layer1(u):
-            pre[u] = bank(u % 3, [P, H])
+            pre[u] = bank(CFG["A"][u], [P, H])
             if u < E:
                 cols = slice(C * (u % 2), C * (u % 2 + 1))
                 nc.tensor.matmul_mx(
@@ -143,7 +155,7 @@ def tile_moe_shf_mlp_relu2_kernel(
                 nc.scalar.activation(rect[u][:], src, ACT.Relu)
 
         def turn(u):
-            turned[u] = bank(3 + u % 3 if u < E else (5, 6, 7, 3)[u - E], [P, 4, P])
+            turned[u] = bank(CFG["B"][u], [P, 4, P])
             for t in range(4):
                 nc.tensor.transpose(turned[u][:, t, :], rect[u][:, t, :], ident[:])
 
@@ -158,35 +170,57 @@ def tile_moe_shf_mlp_relu2_kernel(
             )
 
         def layer2(acc, e, j):
+            g = int(P * j >= CUT)
+            n0 = P * j - g * CUT
             cols = slice(C * (e % 2), C * (e % 2 + 1))
             nc.tensor.matmul_mx(
                 out=acc[:, C * (e % 4) : C * (e % 4 + 1)],
-                lhsT=w2w[e // 4][:, e % 4, 2 * P * j : 2 * P * (j + 1)].bitcast(FP4X4), lhsT_scale=w2c[:, e, P * j : P * (j + 1)],
+                lhsT=w2w[g][:, e, 2 * n0 : 2 * (n0 + P)].bitcast(FP4X4), lhsT_scale=w2c[g][:, e, n0 : n0 + P],
                 rhs=hw[e // 2][:, cols].bitcast(FP8X4), rhs_scale=hc[e // 2][:, cols], start=True, stop=True,
             )
 
         for pair in range(4):
             gather_tokens(pair)
-        for u in range(3):
+        y0_acc = {}
+        cp = [nc.vector.tensor_copy if v else nc.scalar.copy for v in CFG["ye"]]
+
+        def rows0(pair):
+            if not CFG["early"] and pair < 3:
+                return
+            for e in range(2 * pair if CFG["early"] else 0, 2 * pair + 2):
+                g = e // 4 + e // 7
+                if g not in y0_acc:
+                    y0_acc[g] = bank(CFG["y0"][g], [P, 4 * C])
+                layer2(y0_acc[g], e, 0)
+                if e in (3, 6, 7):
+                    c0 = (0, 4, 7)[g]
+                    cp[g](y[0][:, c0 * C : (e + 1) * C], y0_acc[g][:, (c0 % 4) * C : (e % 4 + 1) * C])
+
+        D1 = CFG["d"]
+        for u in range(D1):
             layer1(u)
-        for u in range(3):
-            rectify(u, False)
+        for u in range(D1):
+            rectify(u, CFG["V"][u])
         for u in range(E):
-            layer1(u + 3)
+            ahead = u + D1 < CFG["sh"]
+            if CFG["lfirst"] and ahead:
+                layer1(u + D1)
             turn(u)
+            if not CFG["lfirst"] and ahead:
+                layer1(u + D1)
             square(u)
-            if u >= 5:
-                quantise(u - 5)
+            if u in CFG["q"]:
+                quantise(CFG["q"].index(u))
+                rows0(CFG["q"].index(u))
             if u == E - 1:
                 quantise(3, 0, C)
                 quantise(3, C, 2 * C)
-            rectify(u + 3, True)
-        y0_acc = [bank(6, [P, 4 * C]), bank(7, [P, 4 * C]), bank(3, [P, 4 * C])]
-        for e in range(E):
-            layer2(y0_acc[e // 4 + e // 7], e, 0)
-        nc.scalar.copy(y[0][:, 0 : 4 * C], y0_acc[0][:])
-        nc.vector.tensor_copy(y[0][:, 4 * C : 7 * C], y0_acc[1][:, 0 : 3 * C])
-        nc.scalar.copy(y[0][:, 7 * C : 8 * C], y0_acc[2][:, 3 * C : 4 * C])
+            if ahead:
+                rectify(u + D1, CFG["V"][u + D1])
+        for u in range(min(CFG["sh"], E + D1), max(min(CFG["sh"], E + D1), CFG["sh2"])):
+            layer1(u)
+            rectify(u, CFG["V"][u])
+        rows0(3)
 
         def routed_rows(j, banks):
             for half in range(2):
@@ -239,36 +273,31 @@ def tile_moe_shf_mlp_relu2_kernel(
             nc.scalar.copy(res[:], acc[:].rearrange("p a b -> p (a b)"))
             (nc.scalar if j < 2 else nc.sync).dma_start(out[P * j : P * (j + 1), :], res[:])
 
-        layer1(11)
-        rectify(11, True)
+        for u in range(max(min(CFG["sh"], E + D1), CFG["sh2"]), 12):
+            layer1(u)
+            rectify(u, CFG["V"][u])
         pick(0, 0)
         pick(0, 1)
         for u in range(8, 12):
             turn(u)
             square(u)
         quantise(4)
-        routed_rows(1, (6, 7))
+        routed_rows(1, CFG["y1"])
         pick(1, 0)
         pick(1, 1)
-        routed_rows(2, (3, 6))
-        for j in range(NT):
-            shared_rows(j, (0, 1, 2, 4)[j])
-        park_shared(0)
-        park_shared(1)
-        routed_rows(3, (7, 3))
-        pick(2, 0)
-        sum_turned(0, 5)
-        pick(2, 1)
-        sum_turned(1, 0)
-        park_shared(2)
-        turn_back(0, 1)
-        pick(3, 0)
-        sum_turned(2, 2)
-        turn_back(1, 5)
-        turn_back(2, 6)
+        steps = {
+            "y2": lambda: routed_rows(2, CFG["y2"]), "y3": lambda: routed_rows(3, CFG["y3"]),
+            "ys": lambda: [shared_rows(j, CFG["ys"][j]) for j in range(NT)],
+            "k0": lambda: park_shared(0), "k1": lambda: park_shared(1), "k2": lambda: park_shared(2),
+            "p2": lambda: [pick(2, 0), pick(2, 1)], "p3": lambda: pick(3, 0),
+            "z0": lambda: sum_turned(0, CFG["z"][0]), "z1": lambda: sum_turned(1, CFG["z"][1]), "z2": lambda: sum_turned(2, CFG["z"][2]),
+            "o0": lambda: turn_back(0, CFG["o"][0]), "o1": lambda: turn_back(1, CFG["o"][1]), "o2": lambda: turn_back(2, CFG["o"][2]),
+        }
+        for name in CFG["ord"]:
+            steps[name]()
 
         part = held("part", [P, T], F32)
-        halves = ((0, T // 2), (T // 2, T))
+        halves = ((0, CFG["h"]), (CFG["h"], T))
         pick(3, 1, *halves[0])
         nc.vector.tensor_tensor(part[:], picked[3, 0, 0][:], ys[3][:], ALU.add)
         pick(3, 1, *halves[1])

@@ -19,7 +19,7 @@ ACT = mybir.ActivationFunctionType
 ALU = mybir.AluOpType
 
 P = 128
-CFG = {"A":[6,1,2,3,6,5,0,2,5,0,1,2],"B":[4,7,1,3,4,6,7,4,5,0,7,3],"d":4,"V":[0,0,1,0,1,1,1,1,1,1,1,1],"lfirst":1,"y0":[6,7,3],"ye":[0,1,1],"y1":[4,4],"y2":[3,5],"y3":[5,3],"ys":[4,2,1,0],"z":[7,1,3],"o":[4,2,1],"rb":5,"h":384,"q":[5,6,7],"ord":["ys","k0","k1","k2","z0","y2","z1","y3","o0","p2","z2","p3","o1","o2"],"sh":10,"sh2":12,"n":3,"cut":512,"early":0,"ld":["s1","b","l0","l1","a","s2"]}
+CFG = {"A":[6,1,2,3,6,5,0,2,5,0,1,2],"B":[4,7,1,3,4,6,7,4,5,0,7,3],"d":4,"V":[0,0,1,0,1,1,1,1,1,1,1,1],"lfirst":1,"y0":[6,7,3],"ye":[0,1,1],"y1":[4,4],"y2":[3,5],"y3":[5,3],"ys":[4,2,1,0],"z":[7,1,3,5],"o":[4,2,1,6],"rb":5,"h":384,"q":[5,6,7],"ord":["ys","k0","k1","k2","z0","y2","z1","y3","o0","p2","z2","p3","o1","o2"],"sh":10,"sh2":12,"n":3,"cut":512,"early":0,"ld":["s1","b","l0","l1","a","s2"],"sq":[1,1,0],"half":0,"wt":16,"wm":5}
 NT = N // P
 
 
@@ -179,6 +179,14 @@ def tile_moe_shf_mlp_relu2_kernel(
                 rhs=hw[e // 2][:, cols].bitcast(FP8X4), rhs_scale=hc[e // 2][:, cols], start=True, stop=True,
             )
 
+        idle = bank(0, [P, T])
+        for k in range(CFG["wt"]):
+            nc.tensor.transpose(idle[:, P * (k % 4) : P * (k % 4 + 1)], ident[:], ident[:])
+        for k in range(CFG["wm"]):
+            nc.tensor.matmul_mx(
+                out=idle[:], lhsT=xw[:, 0:P].bitcast(FP8X4), lhsT_scale=xs[:, 0:P],
+                rhs=xw[:].bitcast(FP8X4), rhs_scale=xs[:], start=True, stop=True,
+            )
         for pair in range(4):
             gather_tokens(pair)
         y0_acc = {}
@@ -253,25 +261,25 @@ def tile_moe_shf_mlp_relu2_kernel(
             ys_sb[j] = held("ys_sb%d" % j, [P, T], F32)
             nc.scalar.copy(ys_sb[j][:], ys[j][:])
 
-        def sum_turned(j, b):
+        def sum_turned(j, b, b0=0, b1=4):
             acc = bank(b, [P, 4, P])
             terms = (picked[j, 0, 0], ys_sb[j], picked[j, 1, 0])
-            for tb in range(4):
+            for tb in range(b0, b1):
                 for k, term in enumerate(terms):
                     nc.tensor.matmul(
                         acc[:, tb, :], term[:, P * tb : P * (tb + 1)], ident[:],
                         start=(k == 0), stop=(k == len(terms) - 1), is_transpose=True,
                     )
-            summed[j] = held("summed%d" % j, [P, 4, P], F32)
-            nc.scalar.copy(summed[j][:], acc[:])
+            summed[j, b0] = held("summed%d_%d" % (j, b0), [P, b1 - b0, P], F32)
+            nc.scalar.copy(summed[j, b0][:], acc[:, b0:b1, :])
 
-        def turn_back(j, b):
+        def turn_back(j, b, b0=0, b1=4):
             acc = bank(b, [P, 4, P])
-            for tb in range(4):
-                nc.tensor.transpose(acc[:, tb, :], summed[j][:, tb, :], ident[:])
-            res = held("res%d" % j, [P, T], F32)
-            nc.scalar.copy(res[:], acc[:].rearrange("p a b -> p (a b)"))
-            (nc.scalar if j < 2 else nc.sync).dma_start(out[P * j : P * (j + 1), :], res[:])
+            for tb in range(b0, b1):
+                nc.tensor.transpose(acc[:, tb, :], summed[j, b0][:, tb - b0, :], ident[:])
+            res = held("res%d_%d" % (j, b0), [P, (b1 - b0) * P], F32)
+            nc.scalar.copy(res[:], acc[:, b0:b1, :].rearrange("p a b -> p (a b)"))
+            (nc.scalar if CFG["sq"][j] else nc.sync).dma_start(out[P * j : P * (j + 1), P * b0 : P * b1], res[:])
 
         for u in range(max(min(CFG["sh"], E + D1), CFG["sh2"]), 12):
             layer1(u)
@@ -290,8 +298,8 @@ def tile_moe_shf_mlp_relu2_kernel(
             "ys": lambda: [shared_rows(j, CFG["ys"][j]) for j in range(NT)],
             "k0": lambda: park_shared(0), "k1": lambda: park_shared(1), "k2": lambda: park_shared(2),
             "p2": lambda: [pick(2, 0), pick(2, 1)], "p3": lambda: pick(3, 0),
-            "z0": lambda: sum_turned(0, CFG["z"][0]), "z1": lambda: sum_turned(1, CFG["z"][1]), "z2": lambda: sum_turned(2, CFG["z"][2]),
-            "o0": lambda: turn_back(0, CFG["o"][0]), "o1": lambda: turn_back(1, CFG["o"][1]), "o2": lambda: turn_back(2, CFG["o"][2]),
+            "z0": lambda: sum_turned(0, CFG["z"][0]), "z1": lambda: sum_turned(1, CFG["z"][1]), "z2": lambda: [sum_turned(2, CFG["z"][2], 0, 2), sum_turned(2, CFG["z"][3], 2, 4)] if CFG["half"] else sum_turned(2, CFG["z"][2]),
+            "o0": lambda: turn_back(0, CFG["o"][0]), "o1": lambda: turn_back(1, CFG["o"][1]), "o2": lambda: [turn_back(2, CFG["o"][2], 0, 2), turn_back(2, CFG["o"][3], 2, 4)] if CFG["half"] else turn_back(2, CFG["o"][2]),
         }
         for name in CFG["ord"]:
             steps[name]()

@@ -19,8 +19,11 @@ ACT = mybir.ActivationFunctionType
 ALU = mybir.AluOpType
 
 P = 128
-CFG = {"A":[6,1,2,3,6,5,0,2,5,0,1,2],"B":[4,7,1,3,4,6,7,4,5,0,7,3],"d":4,"V":[0,0,1,0,1,1,1,1,1,1,1,1],"lfirst":1,"y0":[6,7,3],"ye":[0,1,1],"y1":[4,4],"y2":[3,5],"y3":[5,3],"ys":[4,2,1,0],"z":[7,1,3,5],"o":[4,2,1,6],"rb":5,"h":384,"q":[5,6,7],"ord":["ys","k0","k1","k2","z0","y2","z1","y3","o0","p2","z2","p3","o1","o2"],"sh":10,"sh2":12,"n":3,"cut":512,"early":0,"ld":["s1","b","l0","l1","a","s2"],"sq":[1,1,0],"half":0,"wt":16,"wm":5}
+PAIRS = E // 2
+UNITS = E + T // C
 NT = N // P
+RELU_ON_VECTOR = range(4, 10)
+LAST_PIECE = 128
 
 
 def tile_moe_shf_mlp_relu2_kernel(
@@ -30,11 +33,10 @@ def tile_moe_shf_mlp_relu2_kernel(
     nc = tc.nc
     with ExitStack() as ctx:
         keep = ctx.enter_context(tc.tile_pool(name="keep", bufs=1))
-        ring = ctx.enter_context(tc.tile_pool(name="ring", bufs=CFG["rb"]))
         psum = ctx.enter_context(tc.psum_pool(name="psum", bufs=1))
 
-        def held(name, shape, dtype):
-            return keep.tile(shape, dtype, name=name, align_bytes=64)
+        def held(name, shape, dtype, tag=""):
+            return keep.tile(shape, dtype, name=name, tag=tag or name, align_bytes=64)
 
         def bank(b, shape):
             return psum.tile(shape, F32, name="bank%d" % b)
@@ -43,96 +45,73 @@ def tile_moe_shf_mlp_relu2_kernel(
         pos_t = [keep.tile([P, T // 16], U16, name="pos_t%d" % r) for r in range(2)]
         xw = held("xw", [P, T], I32)
         xs = held("xs", [P, T], U8)
-        xgw = [held("xgw%d" % g, [P, 2 * C], U32) for g in range(4)]
-        xgs = [held("xgs%d" % g, [P, 2 * C], U8) for g in range(4)]
-        w1w = [held("w1w%d" % g, [P, 2, 2 * H], U8) for g in range(4)]
+        xgw = [held("xgw%d" % g, [P, 2 * C], U32) for g in range(PAIRS)]
+        xgs = [held("xgs%d" % g, [P, 2 * C], U8) for g in range(PAIRS)]
+        w1w = [held("w1w%d" % g, [P, 2, 2 * H], U8) for g in range(PAIRS)]
         w1c = held("w1c", [P, E, H], U8)
-        CUT = CFG["cut"]
-        w2w = [held("w2w%d" % g, [P, E, 2 * w], U8) for g, w in enumerate((CUT, N - CUT)) if w]
-        w2c = [held("w2c%d" % g, [P, E, w], U8) for g, w in enumerate((CUT, N - CUT)) if w]
+        w2w = held("w2w", [P, E, 2 * N], U8)
+        w2c = held("w2c", [P, E, N], U8)
         w1sw = held("w1sw", [P, HS], I32)
-        w1sc = held("w1sc", [P, HS], U8)
+        w1sc = held("w1sc", [P, 1, HS], U8)
         w2sw = held("w2sw", [P, N], I32)
-        w2sc = held("w2sc", [P, N], U8)
+        w2sc = held("w2sc", [P, 1, N], U8)
         gate_t = held("gate_t", [P, 2, T], F32)
+        ident0 = held("ident0", [P, P], F32)
         ident = held("ident", [P, P], F32)
-        widths = [2 * C] * 4 + [T]
+        widths = [2 * C] * PAIRS + [T]
         hb = [held("hb%d" % g, [P, w, 4], BF16) for g, w in enumerate(widths)]
         hw = [held("hw%d" % g, [P, w], U32) for g, w in enumerate(widths)]
         hc = [held("hc%d" % g, [P, w], U8) for g, w in enumerate(widths)]
         y = [held("y%d" % j, [P, S], F32) for j in range(NT)]
-        warm = held("warm", [P, 8], F32)
-
-        def zero(plane):
-            nc.vector.memset(plane.bitcast(I32), 0)
 
         def load_words(dst, src):
             nc.sync.dma_start(dst[:], src[0].rearrange("p t d -> p (t d)").bitcast(I32))
 
-        def load_plane(dst, src):
+        def load_token_plane(dst, src):
             for q in range(4):
                 rows = src[0, 4 * q : 4 * q + 4, :].bitcast(I32)
                 nc.sync.dma_start(
                     dst[32 * q : 32 * (q + 1), :].bitcast(I32), rows.unsqueeze(0).to_broadcast([8, 4, rows.shape[1]])
                 )
 
-        def load_expert_planes(dst, src, c0, c1):
-            for q in range(4):
-                nc.sync.dma_start(
-                    dst[q:P:32, :, :].bitcast(I32),
-                    src[:, 0, q:16:4, c0:c1].rearrange("e b i -> b e i").bitcast(I32),
-                )
+        def load_planes(dst, src):
+            for r in range(4):
+                nc.sync.dma_start(dst[r:P:32, :, :].bitcast(I32), src[:, r:16:4, :].rearrange("e b i -> b e i").bitcast(I32))
 
         def load_expert_words(dst, src, e0, e1):
-            nc.sync.dma_start(
-                dst[:].bitcast(I32), src[e0:e1, 0].rearrange("e p c -> p e c").bitcast(I32)
-            )
+            nc.sync.dma_start(dst[:].bitcast(I32), src[e0:e1, 0].rearrange("e p c -> p e c").bitcast(I32))
 
-        zero(w1c[:].rearrange("p e i -> p (e i)"))
-        for plane in w2c:
-            zero(plane[:].rearrange("p e i -> p (e i)"))
-        nc.gpsimd.memset(warm[:], 0.0)
-        nc.scalar.activation(warm[:, 4:5], warm[:, 0:1], ACT.Square)
-        make_identity(nc, ident[:])
+        for plane in (w1c, w1sc, w2c, w2sc):
+            nc.vector.memset(plane[:].rearrange("p e i -> p (e i)").bitcast(I32), 0)
+        make_identity(nc, ident0[:])
+        nc.scalar.activation(ident[:], ident0[:], ACT.Relu)
 
-        load_plane(xs, x_scales)
+        load_token_plane(xs, x_scales)
         load_words(xw, x_words)
         nc.sync.dma_start(offs_t[:], offs)
         load_expert_words(w1w[0], w1_words, 0, 2)
-        load_expert_planes(w1c, w1_scales, 0, H)
-        for g in range(1, 4):
+        load_planes(w1c, w1_scales[:, 0])
+        for g in range(1, PAIRS):
             load_expert_words(w1w[g], w1_words, 2 * g, 2 * g + 2)
-        def load_w2(c0, c1):
-            nc.sync.dma_start(
-                w2w[c0 > 0][:].bitcast(I32),
-                w2_words[:, 0, :, 2 * c0 : 2 * c1].rearrange("e p c -> p e c").bitcast(I32),
-            )
-            load_expert_planes(w2c[c0 > 0], w2_scales, c0, c1)
+        load_planes(w1sc, w1s_scales)
+        load_words(w1sw, w1s_words)
+        load_planes(w2c, w2_scales[:, 0])
+        load_expert_words(w2w, w2_words, 0, E)
+        for r, pos in enumerate((pos1, pos2)):
+            nc.sync.dma_start(pos_t[r][:], pos)
+        nc.sync.dma_start(gate_t[:], gate.rearrange("r p t -> p r t"))
+        load_planes(w2sc, w2s_scales)
+        load_words(w2sw, w2s_words)
 
-        def load_list(r):
-            nc.sync.dma_start(pos_t[r][:], (pos1, pos2)[r])
-            nc.sync.dma_start(gate_t[:, r, :], gate[r])
+        pre, rect, turned, acc, picked, ys, ys_sb, zsum, summed, back = ({} for k in range(10))
 
-        loads = {
-            "a": lambda: load_w2(0, CFG["cut"]), "b": lambda: load_w2(CFG["cut"], N) if CFG["cut"] < N else None,
-            "s1": lambda: [load_plane(w1sc, w1s_scales), load_words(w1sw, w1s_words)],
-            "s2": lambda: [load_plane(w2sc, w2s_scales), load_words(w2sw, w2s_words)],
-            "l0": lambda: load_list(0), "l1": lambda: load_list(1),
-        }
-        for name in CFG["ld"]:
-            loads[name]()
+        def gather_tokens(g):
+            lst = offs_t[:, 16 * g : 16 * (g + 1)]
+            nc.vector.tensor_copy(xgw[g][:], xw[:].bitcast(U32).indirect(lst))
+            nc.vector.tensor_copy(xgs[g][:], xs[:].indirect(lst))
 
-        def gather_tokens(pair):
-            lst = offs_t[:, 16 * pair : 16 * (pair + 1)]
-            nc.vector.tensor_copy(xgw[pair][:], xw[:].bitcast(U32).indirect(lst))
-            nc.vector.tensor_copy(xgs[pair][:], xs[:].indirect(lst))
-
-        pre = {}
-        rect = {}
-        turned = {}
-
-        def layer1(u):
-            pre[u] = bank(CFG["A"][u], [P, H])
+        def layer1(u, b):
+            pre[u] = bank(b, [P, H])
             if u < E:
                 cols = slice(C * (u % 2), C * (u % 2 + 1))
                 nc.tensor.matmul_mx(
@@ -143,173 +122,171 @@ def tile_moe_shf_mlp_relu2_kernel(
                 cols = slice(C * (u - E), C * (u - E + 1))
                 nc.tensor.matmul_mx(
                     out=pre[u][:], lhsT=xw[:, cols].bitcast(FP8X4), lhsT_scale=xs[:, cols],
-                    rhs=w1sw[:].bitcast(FP8X4), rhs_scale=w1sc[:], start=True, stop=True,
+                    rhs=w1sw[:].bitcast(FP8X4), rhs_scale=w1sc[:, 0, :], start=True, stop=True,
                 )
 
-        def rectify(u, on_vector):
-            rect[u] = ring.tile([P, 4, P], F32, name="rect")
+        def rectify(u, tag=""):
+            rect[u] = held("rect%d" % u, [P, 4, P], F32, tag)
             src = pre[u][:].rearrange("s (m t) -> s t m", t=4)
-            if on_vector:
+            if u in RELU_ON_VECTOR:
                 nc.vector.tensor_scalar_max(rect[u][:], src, 0.0)
             else:
                 nc.scalar.activation(rect[u][:], src, ACT.Relu)
 
-        def turn(u):
-            turned[u] = bank(CFG["B"][u], [P, 4, P])
+        def turn(u, b):
+            turned[u] = bank(b, [P, 4, P])
             for t in range(4):
                 nc.tensor.transpose(turned[u][:, t, :], rect[u][:, t, :], ident[:])
 
         def square(u):
-            g, k = (u // 2, u % 2) if u < E else (4, u - E)
+            g, k = (u // 2, u % 2) if u < E else (PAIRS, u - E)
             nc.scalar.activation(hb[g][:, C * k : C * (k + 1), :], turned[u][:].rearrange("p t s -> p s t"), ACT.Square)
 
         def quantise(g, c0=0, c1=None):
             nc.vector.quantize_mx(
-                out=hw[g][:, c0:c1].bitcast(FP8X4), scales=hc[g][:, c0:c1],
-                in_=hb[g][:, c0:c1, :].rearrange("p s t -> p (s t)"),
+                out=hw[g][:, c0:c1].bitcast(FP8X4), scales=hc[g][:, c0:c1], in_=hb[g][:, c0:c1, :].rearrange("p s t -> p (s t)")
             )
 
-        def layer2(acc, e, j):
-            g = int(P * j >= CUT)
-            n0 = P * j - g * CUT
-            cols = slice(C * (e % 2), C * (e % 2 + 1))
-            nc.tensor.matmul_mx(
-                out=acc[:, C * (e % 4) : C * (e % 4 + 1)],
-                lhsT=w2w[g][:, e, 2 * n0 : 2 * (n0 + P)].bitcast(FP4X4), lhsT_scale=w2c[g][:, e, n0 : n0 + P],
-                rhs=hw[e // 2][:, cols].bitcast(FP8X4), rhs_scale=hc[e // 2][:, cols], start=True, stop=True,
-            )
+        def layer2(j, e0, e1, b):
+            acc[j, e0] = bank(b, [P, (e1 - e0) * C])
+            for e in range(e0, e1):
+                cols = slice(C * (e % 2), C * (e % 2 + 1))
+                nc.tensor.matmul_mx(
+                    out=acc[j, e0][:, C * (e - e0) : C * (e - e0 + 1)],
+                    lhsT=w2w[:, e, 2 * P * j : 2 * P * (j + 1)].bitcast(FP4X4), lhsT_scale=w2c[:, e, P * j : P * (j + 1)],
+                    rhs=hw[e // 2][:, cols].bitcast(FP8X4), rhs_scale=hc[e // 2][:, cols], start=True, stop=True,
+                )
 
-        idle = bank(0, [P, T])
-        for k in range(CFG["wt"]):
-            nc.tensor.transpose(idle[:, P * (k % 4) : P * (k % 4 + 1)], ident[:], ident[:])
-        for k in range(CFG["wm"]):
-            nc.tensor.matmul_mx(
-                out=idle[:], lhsT=xw[:, 0:P].bitcast(FP8X4), lhsT_scale=xs[:, 0:P],
-                rhs=xw[:].bitcast(FP8X4), rhs_scale=xs[:], start=True, stop=True,
-            )
-        for pair in range(4):
-            gather_tokens(pair)
-        y0_acc = {}
-        cp = [nc.vector.tensor_copy if v else nc.scalar.copy for v in CFG["ye"]]
+        def drain(j, e0, copy=nc.scalar.copy):
+            copy(y[j][:, C * e0 : C * e0 + acc[j, e0].shape[1]], acc[j, e0][:])
 
-        def rows0(pair):
-            if not CFG["early"] and pair < 3:
-                return
-            for e in range(2 * pair if CFG["early"] else 0, 2 * pair + 2):
-                g = e // 4 + e // 7
-                if g not in y0_acc:
-                    y0_acc[g] = bank(CFG["y0"][g], [P, 4 * C])
-                layer2(y0_acc[g], e, 0)
-                if e in (3, 6, 7):
-                    c0 = (0, 4, 7)[g]
-                    cp[g](y[0][:, c0 * C : (e + 1) * C], y0_acc[g][:, (c0 % 4) * C : (e % 4 + 1) * C])
-
-        D1 = CFG["d"]
-        for u in range(D1):
-            layer1(u)
-        for u in range(D1):
-            rectify(u, CFG["V"][u])
-        for u in range(E):
-            ahead = u + D1 < CFG["sh"]
-            if CFG["lfirst"] and ahead:
-                layer1(u + D1)
-            turn(u)
-            if not CFG["lfirst"] and ahead:
-                layer1(u + D1)
-            square(u)
-            if u in CFG["q"]:
-                quantise(CFG["q"].index(u))
-                rows0(CFG["q"].index(u))
-            if u == E - 1:
-                quantise(3, 0, C)
-                quantise(3, C, 2 * C)
-            if ahead:
-                rectify(u + D1, CFG["V"][u + D1])
-        for u in range(min(CFG["sh"], E + D1), max(min(CFG["sh"], E + D1), CFG["sh2"])):
-            layer1(u)
-            rectify(u, CFG["V"][u])
-        rows0(3)
-
-        def routed_rows(j, banks):
-            for half in range(2):
-                acc = bank(banks[half], [P, 4 * C])
-                for e in range(4 * half, 4 * half + 4):
-                    layer2(acc, e, j)
-                nc.scalar.copy(y[j][:, 4 * C * half : 4 * C * (half + 1)], acc[:])
-
-        picked = {}
-
-        def pick(j, r, t0=0, t1=T):
-            picked[j, r, t0] = held("picked%d_%d_%d" % (j, r, t0), [P, t1 - t0], F32)
+        def pick(j, r, t0=0, t1=T, tag=""):
+            picked[j, r, t0] = held("picked%d_%d_%d" % (j, r, t0), [P, t1 - t0], F32, tag)
             nc.vector.tensor_tensor(
                 picked[j, r, t0][:], y[j][:].indirect(pos_t[r][:, t0 // 16 : t1 // 16]), gate_t[:, r, t0:t1], ALU.mult
             )
 
-        ys = {}
-
         def shared_rows(j, b):
             ys[j] = bank(b, [P, T])
             nc.tensor.matmul_mx(
-                out=ys[j][:], lhsT=w2sw[:, P * j : P * (j + 1)].bitcast(FP8X4), lhsT_scale=w2sc[:, P * j : P * (j + 1)],
-                rhs=hw[4][:].bitcast(FP8X4), rhs_scale=hc[4][:], start=True, stop=True,
+                out=ys[j][:], lhsT=w2sw[:, P * j : P * (j + 1)].bitcast(FP8X4), lhsT_scale=w2sc[:, 0, P * j : P * (j + 1)],
+                rhs=hw[PAIRS][:].bitcast(FP8X4), rhs_scale=hc[PAIRS][:], start=True, stop=True,
             )
 
-        ys_sb = {}
-        summed = {}
-
-        def park_shared(j):
+        def park(j):
             ys_sb[j] = held("ys_sb%d" % j, [P, T], F32)
             nc.scalar.copy(ys_sb[j][:], ys[j][:])
 
-        def sum_turned(j, b, b0=0, b1=4):
-            acc = bank(b, [P, 4, P])
-            terms = (picked[j, 0, 0], ys_sb[j], picked[j, 1, 0])
-            for tb in range(b0, b1):
-                for k, term in enumerate(terms):
+        def add_turned(j, b, shared_at):
+            zsum[j] = bank(b, [P, 4, P])
+            terms = [picked[j, 0, 0], picked[j, 1, 0]]
+            terms.insert(shared_at, ys_sb[j])
+            for k, term in enumerate(terms):
+                for tb in range(4):
                     nc.tensor.matmul(
-                        acc[:, tb, :], term[:, P * tb : P * (tb + 1)], ident[:],
-                        start=(k == 0), stop=(k == len(terms) - 1), is_transpose=True,
+                        zsum[j][:, tb, :], term[:, P * tb : P * (tb + 1)], ident[:],
+                        start=(k == 0 and tb == 0), stop=(k == len(terms) - 1 and tb == 3), is_transpose=True,
                     )
-            summed[j, b0] = held("summed%d_%d" % (j, b0), [P, b1 - b0, P], F32)
-            nc.scalar.copy(summed[j, b0][:], acc[:, b0:b1, :])
 
-        def turn_back(j, b, b0=0, b1=4):
-            acc = bank(b, [P, 4, P])
-            for tb in range(b0, b1):
-                nc.tensor.transpose(acc[:, tb, :], summed[j, b0][:, tb - b0, :], ident[:])
-            res = held("res%d_%d" % (j, b0), [P, (b1 - b0) * P], F32)
-            nc.scalar.copy(res[:], acc[:, b0:b1, :].rearrange("p a b -> p (a b)"))
-            (nc.scalar if CFG["sq"][j] else nc.sync).dma_start(out[P * j : P * (j + 1), P * b0 : P * b1], res[:])
+        def drain_sum(j):
+            summed[j] = held("summed%d" % j, [P, 4, P], F32)
+            nc.scalar.copy(summed[j][:], zsum[j][:])
 
-        for u in range(max(min(CFG["sh"], E + D1), CFG["sh2"]), 12):
-            layer1(u)
-            rectify(u, CFG["V"][u])
+        def turn_back(j, b):
+            back[j] = bank(b, [P, 4, P])
+            for tb in range(4):
+                nc.tensor.transpose(back[j][:, tb, :], summed[j][:, tb, :], ident[:])
+
+        def store(j, queue):
+            res = held("res%d" % j, [P, T], F32)
+            nc.scalar.copy(res[:], back[j][:].rearrange("p a b -> p (a b)"))
+            queue.dma_start(out[P * j : P * (j + 1), :], res[:])
+
+        for g in range(PAIRS):
+            gather_tokens(g)
+        for u in range(4):
+            layer1(u, u)
+        for u in range(4):
+            rectify(u)
+        turn(0, 4)
+        turn(1, 0)
+        layer1(4, 1)
+        layer1(5, 2)
+        turn(2, 5)
+        turn(3, 6)
+        layer1(6, 3)
+        square(0)
+        layer1(7, 4)
+        for u in range(1, 4):
+            square(u)
+        for u in range(4, 8):
+            rectify(u)
+        for u, b in zip(range(4, 8), (7, 0, 5, 6)):
+            turn(u, b)
+            square(u)
+        for u in range(E, UNITS):
+            layer1(u, u - E + 1)
+        quantise(0)
+        quantise(1)
+        quantise(2)
+        rectify(8)
+        quantise(3, 0, C)
+        quantise(3, C, 2 * C)
+        rectify(9, "hb3")
+        rectify(10)
+        rectify(11)
+        layer2(0, 0, 4, 7)
+        layer2(0, 4, 8, 0)
+        drain(0, 0)
+        drain(0, 4, nc.vector.tensor_copy)
+        layer2(1, 0, 4, 5)
+        layer2(1, 4, 8, 6)
+        drain(1, 0)
+        drain(1, 4)
         pick(0, 0)
         pick(0, 1)
-        for u in range(8, 12):
-            turn(u)
-            square(u)
-        quantise(4)
-        routed_rows(1, CFG["y1"])
         pick(1, 0)
-        pick(1, 1)
-        steps = {
-            "y2": lambda: routed_rows(2, CFG["y2"]), "y3": lambda: routed_rows(3, CFG["y3"]),
-            "ys": lambda: [shared_rows(j, CFG["ys"][j]) for j in range(NT)],
-            "k0": lambda: park_shared(0), "k1": lambda: park_shared(1), "k2": lambda: park_shared(2),
-            "p2": lambda: [pick(2, 0), pick(2, 1)], "p3": lambda: pick(3, 0),
-            "z0": lambda: sum_turned(0, CFG["z"][0]), "z1": lambda: sum_turned(1, CFG["z"][1]), "z2": lambda: [sum_turned(2, CFG["z"][2], 0, 2), sum_turned(2, CFG["z"][3], 2, 4)] if CFG["half"] else sum_turned(2, CFG["z"][2]),
-            "o0": lambda: turn_back(0, CFG["o"][0]), "o1": lambda: turn_back(1, CFG["o"][1]), "o2": lambda: [turn_back(2, CFG["o"][2], 0, 2), turn_back(2, CFG["o"][3], 2, 4)] if CFG["half"] else turn_back(2, CFG["o"][2]),
-        }
-        for name in CFG["ord"]:
-            steps[name]()
+        for u, b in zip(range(E, UNITS), (7, 0, 5, 6)):
+            turn(u, b)
+            square(u)
+        quantise(PAIRS)
+        pick(1, 1, tag="hb4")
+        layer2(2, 0, 4, 1)
+        layer2(2, 4, 8, 2)
+        drain(2, 0)
+        drain(2, 4)
+        layer2(3, 0, 4, 3)
+        layer2(3, 4, 8, 4)
+        drain(3, 0)
+        drain(3, 4)
+        for j, b in enumerate((5, 6, 1, 2)):
+            shared_rows(j, b)
+        pick(2, 0)
+        pick(2, 1)
+        park(0)
+        park(1)
+        add_turned(0, 7, 2)
+        add_turned(1, 0, 2)
+        drain_sum(0)
+        drain_sum(1)
+        park(2)
+        turn_back(0, 5)
+        turn_back(1, 4)
+        add_turned(2, 6, 1)
+        drain_sum(2)
+        store(0, nc.scalar)
+        store(1, nc.scalar)
+        turn_back(2, 3)
+        store(2, nc.sync)
 
+        j = NT - 1
+        cut = T - LAST_PIECE
         part = held("part", [P, T], F32)
-        halves = ((0, CFG["h"]), (CFG["h"], T))
-        pick(3, 1, *halves[0])
-        nc.vector.tensor_tensor(part[:], picked[3, 0, 0][:], ys[3][:], ALU.add)
-        pick(3, 1, *halves[1])
-        for t0, t1 in halves:
+        pick(j, 0)
+        pick(j, 1, 0, cut)
+        nc.vector.tensor_tensor(part[:], picked[j, 0, 0][:], ys[j][:], ALU.add)
+        pick(j, 1, cut, T)
+        for t0, t1 in ((0, cut), (cut, T)):
             res = held("res3_%d" % t0, [P, t1 - t0], F32)
-            nc.vector.tensor_tensor(res[:], part[:, t0:t1], picked[3, 1, t0][:], ALU.add)
-            nc.sync.dma_start(out[P * 3 : P * 4, t0:t1], res[:])
+            nc.vector.tensor_tensor(res[:], part[:, t0:t1], picked[j, 1, t0][:], ALU.add)
+            nc.sync.dma_start(out[P * j : P * (j + 1), t0:t1], res[:])

@@ -202,6 +202,12 @@ def tile_moe_shf_mlp_relu2_kernel(
             nc.scalar.copy(res[:], back[j][:].rearrange("p a b -> p (a b)"))
             queue.dma_start(out[P * j : P * (j + 1), :], res[:])
 
+        idle = bank(7, [P, T])
+        for k in range(4):
+            nc.tensor.matmul_mx(
+                out=idle[:], lhsT=xw[:, 0:P].bitcast(FP8X4), lhsT_scale=xs[:, 0:P],
+                rhs=xw[:].bitcast(FP8X4), rhs_scale=xs[:], start=True, stop=True,
+            )
         for g in range(PAIRS):
             gather_tokens(g)
         for u in range(4):

@@ -22,7 +22,7 @@ P = 128
 PAIRS = E // 2
 UNITS = E + T // C
 NT = N // P
-RELU_ON_VECTOR = range(4, 10)
+RELU_ON_VECTOR = range(4, 11)
 LAST_PIECE = 128
 
 
@@ -227,72 +227,82 @@ def tile_moe_shf_mlp_relu2_kernel(
             square(u)
         for u in range(4, 8):
             rectify(u)
-        for u, b in zip(range(4, 8), (7, 0, 5, 6)):
-            turn(u, b)
+        turn(4, 7)
+        turn(5, 0)
+        layer1(8, 1)
+        layer1(9, 2)
+        turn(6, 5)
+        turn(7, 6)
+        layer1(10, 3)
+        for u in range(4, 8):
             square(u)
-        for u in range(E, UNITS):
-            layer1(u, u - E + 1)
         quantise(0)
         quantise(1)
-        quantise(2)
         rectify(8)
+        quantise(2)
         quantise(3, 0, C)
+        rectify(9, "hb2")
         quantise(3, C, 2 * C)
-        rectify(9, "hb3")
-        rectify(10)
-        rectify(11)
+        rectify(10, "hb3")
         layer2(0, 0, 4, 7)
-        layer2(0, 4, 8, 0)
+        layer2(0, 4, 7, 0)
+        layer2(0, 7, 8, 4)
         drain(0, 0)
-        drain(0, 4, nc.vector.tensor_copy)
+        drain(0, 4)
+        drain(0, 7, nc.vector.tensor_copy)
         layer2(1, 0, 4, 5)
         layer2(1, 4, 8, 6)
+        layer1(11, 4)
         drain(1, 0)
         drain(1, 4)
+        rectify(11)
         pick(0, 0)
         pick(0, 1)
         pick(1, 0)
+        pick(1, 1)
         for u, b in zip(range(E, UNITS), (7, 0, 5, 6)):
             turn(u, b)
             square(u)
         quantise(PAIRS)
-        pick(1, 1, tag="hb4")
-        layer2(2, 0, 4, 1)
-        layer2(2, 4, 8, 2)
-        drain(2, 0)
-        drain(2, 4)
-        layer2(3, 0, 4, 3)
-        layer2(3, 4, 8, 4)
-        drain(3, 0)
-        drain(3, 4)
-        for j, b in enumerate((5, 6, 1, 2)):
+        layer2(2, 0, 4, 7)
+        layer2(2, 4, 8, 0)
+        layer2(3, 0, 4, 5)
+        layer2(3, 4, 8, 6)
+        for j in (2, 3):
+            drain(j, 0)
+            drain(j, 4)
+        for j, b in enumerate((1, 2, 3, 4)):
             shared_rows(j, b)
-        pick(2, 0)
-        pick(2, 1)
         park(0)
         park(1)
         add_turned(0, 7, 2)
         add_turned(1, 0, 2)
         drain_sum(0)
         drain_sum(1)
-        park(2)
         turn_back(0, 5)
-        turn_back(1, 4)
-        add_turned(2, 6, 1)
-        drain_sum(2)
+        turn_back(1, 6)
         store(0, nc.scalar)
         store(1, nc.scalar)
-        turn_back(2, 3)
-        store(2, nc.sync)
 
-        j = NT - 1
-        cut = T - LAST_PIECE
-        part = held("part", [P, T], F32)
-        pick(j, 0)
-        pick(j, 1, 0, cut)
-        nc.vector.tensor_tensor(part[:], picked[j, 0, 0][:], ys[j][:], ALU.add)
-        pick(j, 1, cut, T)
-        for t0, t1 in ((0, cut), (cut, T)):
-            res = held("res3_%d" % t0, [P, t1 - t0], F32)
-            nc.vector.tensor_tensor(res[:], part[:, t0:t1], picked[j, 1, t0][:], ALU.add)
+        part = {}
+
+        def add_shared(j):
+            part[j] = held("part%d" % j, [P, T], F32)
+            nc.vector.tensor_tensor(part[j][:], picked[j, 0, 0][:], ys[j][:], ALU.add)
+
+        def finish(j, t0, t1):
+            res = held("res%d_%d" % (j, t0), [P, t1 - t0], F32)
+            nc.vector.tensor_tensor(res[:], part[j][:, t0:t1], picked[j, 1, t0][:], ALU.add)
             nc.sync.dma_start(out[P * j : P * (j + 1), t0:t1], res[:])
+
+        cut = T - LAST_PIECE
+        pick(2, 0)
+        pick(2, 1)
+        add_shared(2)
+        pick(3, 0)
+        finish(2, 0, T)
+        pick(3, 1, 0, cut)
+        add_shared(3)
+        pick(3, 1, cut, T)
+        finish(3, 0, cut)
+        finish(3, cut, T)

@@ -22,7 +22,7 @@ P = 128
 PAIRS = E // 2
 UNITS = E + T // C
 NT = N // P
-RELU_ON_VECTOR = range(4, 11)
+RELU_ON_VECTOR = (4, 5, 6, 7, 8, 9, 11)
 LAST_PIECE = 128
 
 
@@ -173,37 +173,40 @@ def tile_moe_shf_mlp_relu2_kernel(
                 rhs=hw[PAIRS][:].bitcast(FP8X4), rhs_scale=hc[PAIRS][:], start=True, stop=True,
             )
 
-        def park(j):
-            ys_sb[j] = held("ys_sb%d" % j, [P, T], F32)
-            nc.scalar.copy(ys_sb[j][:], ys[j][:])
+        def park(j, blocks=4):
+            ys_sb[j] = held("ys_sb%d" % j, [P, P * blocks], F32)
+            nc.scalar.copy(ys_sb[j][:], ys[j][:, 0 : P * blocks])
 
-        def add_turned(j, b, shared_at):
+        def add_turned(j, term, first, last):
+            blocks = zsum[j].shape[1]
+            for tb in range(blocks):
+                nc.tensor.matmul(
+                    zsum[j][:, tb, :], term[:, P * tb : P * (tb + 1)], ident[:],
+                    start=(first and tb == 0), stop=(last and tb == blocks - 1), is_transpose=True,
+                )
+
+        def add_routed(j, b):
             zsum[j] = bank(b, [P, 4, P])
-            terms = [picked[j, 0, 0], picked[j, 1, 0]]
-            terms.insert(shared_at, ys_sb[j])
-            for k, term in enumerate(terms):
-                for tb in range(4):
-                    nc.tensor.matmul(
-                        zsum[j][:, tb, :], term[:, P * tb : P * (tb + 1)], ident[:],
-                        start=(k == 0 and tb == 0), stop=(k == len(terms) - 1 and tb == 3), is_transpose=True,
-                    )
+            add_turned(j, picked[j, 0, 0], True, False)
+            add_turned(j, picked[j, 1, 0], False, False)
 
         def drain_sum(j):
-            summed[j] = held("summed%d" % j, [P, 4, P], F32)
+            summed[j] = held("summed%d" % j, zsum[j].shape, F32)
             nc.scalar.copy(summed[j][:], zsum[j][:])
 
         def turn_back(j, b):
-            back[j] = bank(b, [P, 4, P])
-            for tb in range(4):
+            back[j] = bank(b, zsum[j].shape)
+            for tb in range(zsum[j].shape[1]):
                 nc.tensor.transpose(back[j][:, tb, :], summed[j][:, tb, :], ident[:])
 
         def store(j, queue):
-            res = held("res%d" % j, [P, T], F32)
+            width = P * zsum[j].shape[1]
+            res = held("res%d" % j, [P, width], F32)
             nc.scalar.copy(res[:], back[j][:].rearrange("p a b -> p (a b)"))
-            queue.dma_start(out[P * j : P * (j + 1), :], res[:])
+            queue.dma_start(out[P * j : P * (j + 1), 0:width], res[:])
 
         idle = bank(7, [P, T])
-        for k in range(4):
+        for k in range(3):
             nc.tensor.matmul_mx(
                 out=idle[:], lhsT=xw[:, 0:P].bitcast(FP8X4), lhsT_scale=xs[:, 0:P],
                 rhs=xw[:].bitcast(FP8X4), rhs_scale=xs[:], start=True, stop=True,
@@ -234,6 +237,7 @@ def tile_moe_shf_mlp_relu2_kernel(
         turn(6, 5)
         turn(7, 6)
         layer1(10, 3)
+        layer1(11, 4)
         for u in range(4, 8):
             square(u)
         quantise(0)
@@ -241,21 +245,20 @@ def tile_moe_shf_mlp_relu2_kernel(
         rectify(8)
         quantise(2)
         quantise(3, 0, C)
-        rectify(9, "hb2")
+        rectify(9)
         quantise(3, C, 2 * C)
-        rectify(10, "hb3")
+        rectify(10)
+        rectify(11, "hb3")
         layer2(0, 0, 4, 7)
         layer2(0, 4, 7, 0)
-        layer2(0, 7, 8, 4)
+        layer2(0, 7, 8, 1)
         drain(0, 0)
         drain(0, 4)
         drain(0, 7, nc.vector.tensor_copy)
         layer2(1, 0, 4, 5)
         layer2(1, 4, 8, 6)
-        layer1(11, 4)
         drain(1, 0)
         drain(1, 4)
-        rectify(11)
         pick(0, 0)
         pick(0, 1)
         pick(1, 0)
@@ -271,38 +274,49 @@ def tile_moe_shf_mlp_relu2_kernel(
         for j in (2, 3):
             drain(j, 0)
             drain(j, 4)
+        add_routed(0, 7)
         for j, b in enumerate((1, 2, 3, 4)):
             shared_rows(j, b)
+        add_routed(1, 0)
+        pick(2, 0)
+        pick(2, 1)
         park(0)
         park(1)
-        add_turned(0, 7, 2)
-        add_turned(1, 0, 2)
+        add_turned(0, ys_sb[0], False, True)
+        add_turned(1, ys_sb[1], False, True)
         drain_sum(0)
+        park(2, 2)
         drain_sum(1)
         turn_back(0, 5)
         turn_back(1, 6)
+        zsum[2] = bank(2, [P, 2, P])
+        add_turned(2, picked[2, 0, 0], True, False)
+        add_turned(2, ys_sb[2], False, False)
+        add_turned(2, picked[2, 1, 0], False, True)
         store(0, nc.scalar)
+        drain_sum(2)
         store(1, nc.scalar)
+        turn_back(2, 1)
+        store(2, nc.sync)
 
         part = {}
 
-        def add_shared(j):
-            part[j] = held("part%d" % j, [P, T], F32)
-            nc.vector.tensor_tensor(part[j][:], picked[j, 0, 0][:], ys[j][:], ALU.add)
+        def add_shared(j, t0):
+            part[j] = held("part%d" % j, [P, T - t0], F32)
+            nc.vector.tensor_tensor(part[j][:], picked[j, 0, 0][:, t0:T], ys[j][:, t0:T], ALU.add)
 
-        def finish(j, t0, t1):
-            res = held("res%d_%d" % (j, t0), [P, t1 - t0], F32)
-            nc.vector.tensor_tensor(res[:], part[j][:, t0:t1], picked[j, 1, t0][:], ALU.add)
-            nc.sync.dma_start(out[P * j : P * (j + 1), t0:t1], res[:])
+        def finish(j, first, second, t0):
+            width = first.shape[1]
+            res = held("res%d_%d" % (j, t0), [P, width], F32)
+            nc.vector.tensor_tensor(res[:], first, second, ALU.add)
+            nc.sync.dma_start(out[P * j : P * (j + 1), t0 : t0 + width], res[:])
 
         cut = T - LAST_PIECE
-        pick(2, 0)
-        pick(2, 1)
-        add_shared(2)
         pick(3, 0)
-        finish(2, 0, T)
+        add_shared(2, 256)
         pick(3, 1, 0, cut)
-        add_shared(3)
+        finish(2, part[2][:], picked[2, 1, 0][:, 256:T], 256)
+        add_shared(3, 0)
         pick(3, 1, cut, T)
-        finish(3, 0, cut)
-        finish(3, cut, T)
+        finish(3, part[3][:, 0:cut], picked[3, 1, 0][:], 0)
+        finish(3, part[3][:, cut:T], picked[3, 1, cut][:], cut)

@@ -103,7 +103,7 @@ def tile_moe_shf_mlp_relu2_kernel(
         load_planes(w2sc, w2s_scales)
         load_words(w2sw, w2s_words)
 
-        pre, rect, turned, acc, picked, ys, ys_sb, zsum, summed, back = ({} for k in range(10))
+        pre, rect, turned, acc, picked, ys, ys_sb, zsum, summed, back, result = ({} for k in range(11))
 
         def gather_tokens(g):
             lst = offs_t[:, 16 * g : 16 * (g + 1)]
@@ -199,11 +199,12 @@ def tile_moe_shf_mlp_relu2_kernel(
             for tb in range(zsum[j].shape[1]):
                 nc.tensor.transpose(back[j][:, tb, :], summed[j][:, tb, :], ident[:])
 
+        def drain_back(j):
+            result[j] = held("res%d" % j, [P, P * zsum[j].shape[1]], F32)
+            nc.scalar.copy(result[j][:], back[j][:].rearrange("p a b -> p (a b)"))
+
         def store(j, queue):
-            width = P * zsum[j].shape[1]
-            res = held("res%d" % j, [P, width], F32)
-            nc.scalar.copy(res[:], back[j][:].rearrange("p a b -> p (a b)"))
-            queue.dma_start(out[P * j : P * (j + 1), 0:width], res[:])
+            queue.dma_start(out[P * j : P * (j + 1), 0 : result[j].shape[1]], result[j][:])
 
         idle = bank(7, [P, T])
         for k in range(3):
@@ -275,48 +276,38 @@ def tile_moe_shf_mlp_relu2_kernel(
             drain(j, 0)
             drain(j, 4)
         add_routed(0, 7)
+        add_routed(1, 0)
         for j, b in enumerate((1, 2, 3, 4)):
             shared_rows(j, b)
-        add_routed(1, 0)
         pick(2, 0)
         pick(2, 1)
         park(0)
         park(1)
         add_turned(0, ys_sb[0], False, True)
         add_turned(1, ys_sb[1], False, True)
-        drain_sum(0)
-        park(2, 2)
-        drain_sum(1)
-        turn_back(0, 5)
-        turn_back(1, 6)
-        zsum[2] = bank(2, [P, 2, P])
+        park(2, 4)
+        zsum[2] = bank(2, [P, 4, P])
         add_turned(2, picked[2, 0, 0], True, False)
         add_turned(2, ys_sb[2], False, False)
         add_turned(2, picked[2, 1, 0], False, True)
+        for j, b in enumerate((5, 6, 1)):
+            drain_sum(j)
+            turn_back(j, b)
+        drain_back(0)
+        drain_back(1)
         store(0, nc.scalar)
-        drain_sum(2)
+        drain_back(2)
         store(1, nc.scalar)
-        turn_back(2, 1)
         store(2, nc.sync)
 
-        part = {}
-
-        def add_shared(j, t0):
-            part[j] = held("part%d" % j, [P, T - t0], F32)
-            nc.vector.tensor_tensor(part[j][:], picked[j, 0, 0][:, t0:T], ys[j][:, t0:T], ALU.add)
-
-        def finish(j, first, second, t0):
-            width = first.shape[1]
-            res = held("res%d_%d" % (j, t0), [P, width], F32)
-            nc.vector.tensor_tensor(res[:], first, second, ALU.add)
-            nc.sync.dma_start(out[P * j : P * (j + 1), t0 : t0 + width], res[:])
-
-        cut = T - LAST_PIECE
-        pick(3, 0)
-        add_shared(2, 256)
-        pick(3, 1, 0, cut)
-        finish(2, part[2][:], picked[2, 1, 0][:, 256:T], 256)
-        add_shared(3, 0)
-        pick(3, 1, cut, T)
-        finish(3, part[3][:, 0:cut], picked[3, 1, 0][:], 0)
-        finish(3, part[3][:, cut:T], picked[3, 1, cut][:], cut)
+        j = NT - 1
+        pieces = ((0, T - LAST_PIECE), (T - LAST_PIECE, T))
+        part = held("part", [P, T], F32)
+        pick(j, 0)
+        pick(j, 1)
+        for t0, t1 in pieces:
+            nc.vector.tensor_tensor(part[:, t0:t1], picked[j, 0, 0][:, t0:t1], ys[j][:, t0:t1], ALU.add)
+        for t0, t1 in pieces:
+            res = held("res3_%d" % t0, [P, t1 - t0], F32)
+            nc.vector.tensor_tensor(res[:], part[:, t0:t1], picked[j, 1, 0][:, t0:t1], ALU.add)
+            nc.sync.dma_start(out[P * j : P * (j + 1), t0:t1], res[:])

@@ -173,16 +173,15 @@ def tile_moe_shf_mlp_relu2_kernel(
                 rhs=hw[PAIRS][:].bitcast(FP8X4), rhs_scale=hc[PAIRS][:], start=True, stop=True,
             )
 
-        def park(j, blocks=4):
-            ys_sb[j] = held("ys_sb%d" % j, [P, P * blocks], F32)
-            nc.scalar.copy(ys_sb[j][:], ys[j][:, 0 : P * blocks])
+        def park(j):
+            ys_sb[j] = held("ys_sb%d" % j, [P, T], F32)
+            nc.scalar.copy(ys_sb[j][:], ys[j][:])
 
         def add_turned(j, term, first, last):
-            blocks = zsum[j].shape[1]
-            for tb in range(blocks):
+            for tb in range(4):
                 nc.tensor.matmul(
                     zsum[j][:, tb, :], term[:, P * tb : P * (tb + 1)], ident[:],
-                    start=(first and tb == 0), stop=(last and tb == blocks - 1), is_transpose=True,
+                    start=(first and tb == 0), stop=(last and tb == 3), is_transpose=True,
                 )
 
         def add_routed(j, b):
@@ -191,20 +190,20 @@ def tile_moe_shf_mlp_relu2_kernel(
             add_turned(j, picked[j, 1, 0], False, False)
 
         def drain_sum(j):
-            summed[j] = held("summed%d" % j, zsum[j].shape, F32)
+            summed[j] = held("summed%d" % j, [P, 4, P], F32)
             nc.scalar.copy(summed[j][:], zsum[j][:])
 
         def turn_back(j, b):
-            back[j] = bank(b, zsum[j].shape)
-            for tb in range(zsum[j].shape[1]):
+            back[j] = bank(b, [P, 4, P])
+            for tb in range(4):
                 nc.tensor.transpose(back[j][:, tb, :], summed[j][:, tb, :], ident[:])
 
         def drain_back(j):
-            result[j] = held("res%d" % j, [P, P * zsum[j].shape[1]], F32)
+            result[j] = held("res%d" % j, [P, T], F32)
             nc.scalar.copy(result[j][:], back[j][:].rearrange("p a b -> p (a b)"))
 
         def store(j, queue):
-            queue.dma_start(out[P * j : P * (j + 1), 0 : result[j].shape[1]], result[j][:])
+            queue.dma_start(out[P * j : P * (j + 1), :], result[j][:])
 
         idle = bank(7, [P, T])
         for k in range(3):
@@ -263,7 +262,6 @@ def tile_moe_shf_mlp_relu2_kernel(
         pick(0, 0)
         pick(0, 1)
         pick(1, 0)
-        pick(1, 1)
         for u, b in zip(range(E, UNITS), (7, 0, 5, 6)):
             turn(u, b)
             square(u)
@@ -272,11 +270,11 @@ def tile_moe_shf_mlp_relu2_kernel(
         layer2(2, 4, 8, 0)
         layer2(3, 0, 4, 5)
         layer2(3, 4, 8, 6)
+        pick(1, 1, tag="hw2")
         for j in (2, 3):
             drain(j, 0)
             drain(j, 4)
         add_routed(0, 7)
-        add_routed(1, 0)
         for j, b in enumerate((1, 2, 3, 4)):
             shared_rows(j, b)
         pick(2, 0)
@@ -284,8 +282,9 @@ def tile_moe_shf_mlp_relu2_kernel(
         park(0)
         park(1)
         add_turned(0, ys_sb[0], False, True)
+        add_routed(1, 0)
         add_turned(1, ys_sb[1], False, True)
-        park(2, 4)
+        park(2)
         zsum[2] = bank(2, [P, 4, P])
         add_turned(2, picked[2, 0, 0], True, False)
         add_turned(2, ys_sb[2], False, False)
@@ -301,13 +300,13 @@ def tile_moe_shf_mlp_relu2_kernel(
         store(2, nc.sync)
 
         j = NT - 1
-        pieces = ((0, T - LAST_PIECE), (T - LAST_PIECE, T))
+        cut = T - LAST_PIECE
         part = held("part", [P, T], F32)
         pick(j, 0)
-        pick(j, 1)
-        for t0, t1 in pieces:
-            nc.vector.tensor_tensor(part[:, t0:t1], picked[j, 0, 0][:, t0:t1], ys[j][:, t0:t1], ALU.add)
-        for t0, t1 in pieces:
+        pick(j, 1, 0, cut)
+        nc.vector.tensor_tensor(part[:], picked[j, 0, 0][:], ys[j][:], ALU.add)
+        pick(j, 1, cut, T)
+        for t0, t1 in ((0, cut), (cut, T)):
             res = held("res3_%d" % t0, [P, t1 - t0], F32)
-            nc.vector.tensor_tensor(res[:], part[:, t0:t1], picked[j, 1, 0][:, t0:t1], ALU.add)
+            nc.vector.tensor_tensor(res[:], part[:, t0:t1], picked[j, 1, t0][:], ALU.add)
             nc.sync.dma_start(out[P * j : P * (j + 1), t0:t1], res[:])

@@ -189,8 +189,8 @@ def tile_moe_shf_mlp_relu2_kernel(
             add_turned(j, picked[j, 0, 0], True, False)
             add_turned(j, picked[j, 1, 0], False, False)
 
-        def drain_sum(j):
-            summed[j] = held("summed%d" % j, [P, 4, P], F32)
+        def drain_sum(j, tag=""):
+            summed[j] = held("summed%d" % j, [P, 4, P], F32, tag)
             nc.scalar.copy(summed[j][:], zsum[j][:])
 
         def turn_back(j, b):
@@ -288,16 +288,19 @@ def tile_moe_shf_mlp_relu2_kernel(
         zsum[2] = bank(2, [P, 4, P])
         add_turned(2, picked[2, 0, 0], True, False)
         add_turned(2, ys_sb[2], False, False)
+        drain_sum(0, "summed_a")
+        turn_back(0, 5)
         add_turned(2, picked[2, 1, 0], False, True)
-        for j, b in enumerate((5, 6, 1)):
-            drain_sum(j)
-            turn_back(j, b)
+        drain_sum(1)
+        turn_back(1, 6)
         drain_back(0)
+        drain_sum(2, "summed_a")
+        turn_back(2, 1)
         drain_back(1)
         store(0, nc.scalar)
-        drain_back(2)
         store(1, nc.scalar)
-        store(2, nc.sync)
+        drain_back(2)
+        store(2, nc.scalar)
 
         j = NT - 1
         cut = T - LAST_PIECE

@@ -70,7 +70,7 @@ def tile_moe_shf_mlp_relu2_kernel(
         def load_token_plane(dst, src):
             for q in range(4):
                 rows = src[0, 4 * q : 4 * q + 4, :].bitcast(I32)
-                nc.sync.dma_start(
+                (nc.sync if q < 2 else nc.scalar).dma_start(
                     dst[32 * q : 32 * (q + 1), :].bitcast(I32), rows.unsqueeze(0).to_broadcast([8, 4, rows.shape[1]])
                 )
 

@@ -22,6 +22,10 @@ P = 128
 PAIRS = E // 2
 UNITS = E + T // C
 NT = N // P
+GATHERS = ((0, 2), (2, 4), (4, 6), (6, 8))
+W1_LOADS = ((0, 2), (2, 4), (4, 6), (6, 8))
+W1_PLANES = ((0, 4), (4, 8))
+HIDDEN = ((0, 2), (2, 4), (4, 6), (6, 8), (8, 12))
 RELU_ON_VECTOR = (4, 5, 6, 7, 8, 9, 11)
 LAST_PIECE = 128
 
@@ -45,10 +49,10 @@ def tile_moe_shf_mlp_relu2_kernel(
         pos_t = [keep.tile([P, T // 16], U16, name="pos_t%d" % r) for r in range(2)]
         xw = held("xw", [P, T], I32)
         xs = held("xs", [P, T], U8)
-        xgw = [held("xgw%d" % g, [P, 2 * C], U32) for g in range(PAIRS)]
-        xgs = [held("xgs%d" % g, [P, 2 * C], U8) for g in range(PAIRS)]
-        w1w = [held("w1w%d" % g, [P, 2, 2 * H], U8) for g in range(PAIRS)]
-        w1c = held("w1c", [P, E, H], U8)
+        xgw = [held("xgw%d" % e0, [P, (e1 - e0) * C], U32) for e0, e1 in GATHERS]
+        xgs = [held("xgs%d" % e0, [P, (e1 - e0) * C], U8) for e0, e1 in GATHERS]
+        w1w = [held("w1w%d" % e0, [P, e1 - e0, 2 * H], U8) for e0, e1 in W1_LOADS]
+        w1c = [held("w1c%d" % e0, [P, e1 - e0, H], U8) for e0, e1 in W1_PLANES]
         w2w = held("w2w", [P, E, 2 * N], U8)
         w2c = held("w2c", [P, E, N], U8)
         w1sw = held("w1sw", [P, HS], I32)
@@ -58,42 +62,44 @@ def tile_moe_shf_mlp_relu2_kernel(
         gate_t = held("gate_t", [P, 2, T], F32)
         ident0 = held("ident0", [P, P], F32)
         ident = held("ident", [P, P], F32)
-        widths = [2 * C] * PAIRS + [T]
-        hb = [held("hb%d" % g, [P, w, 4], BF16) for g, w in enumerate(widths)]
-        hw = [held("hw%d" % g, [P, w], U32) for g, w in enumerate(widths)]
-        hc = [held("hc%d" % g, [P, w], U8) for g, w in enumerate(widths)]
-        y = [held("y%d" % j, [P, S], F32) for j in range(NT)]
+        hb = [held("hb%d" % u0, [P, (u1 - u0) * C, 4], BF16) for u0, u1 in HIDDEN]
+        hc = [held("hc%d" % u0, [P, (u1 - u0) * C], U8) for u0, u1 in HIDDEN]
+        hw, y = {}, {}
 
-        def load_words(dst, src):
-            nc.sync.dma_start(dst[:], src[0].rearrange("p t d -> p (t d)").bitcast(I32))
+        def place(groups, u):
+            g = [u0 <= u < u1 for u0, u1 in groups].index(True)
+            return g, u - groups[g][0]
 
-        def load_token_plane(dst, src):
-            for q in range(4):
-                rows = src[0, 4 * q : 4 * q + 4, :].bitcast(I32)
-                (nc.sync if q < 2 else nc.scalar).dma_start(
-                    dst[32 * q : 32 * (q + 1), :].bitcast(I32), rows.unsqueeze(0).to_broadcast([8, 4, rows.shape[1]])
-                )
+        def load_words(dst, src, queue=nc.sync):
+            queue.dma_start(dst[:], src[0].rearrange("p t d -> p (t d)").bitcast(I32))
 
-        def load_planes(dst, src):
+        def load_token_rows(q, queue):
+            rows = x_scales[0, 4 * q : 4 * q + 4, :].bitcast(I32)
+            queue.dma_start(xs[32 * q : 32 * (q + 1), :].bitcast(I32), rows.unsqueeze(0).to_broadcast([8, 4, rows.shape[1]]))
+
+        def load_planes(dst, src, queue=nc.sync):
             for r in range(4):
-                nc.sync.dma_start(dst[r:P:32, :, :].bitcast(I32), src[:, r:16:4, :].rearrange("e b i -> b e i").bitcast(I32))
+                queue.dma_start(dst[r:P:32, :, :].bitcast(I32), src[:, r:16:4, :].rearrange("e b i -> b e i").bitcast(I32))
 
         def load_expert_words(dst, src, e0, e1):
             nc.sync.dma_start(dst[:].bitcast(I32), src[e0:e1, 0].rearrange("e p c -> p e c").bitcast(I32))
 
-        for plane in (w1c, w1sc, w2c, w2sc):
+        for plane in (w1c[0], w1sc, w1c[1], w2c, w2sc):
             nc.vector.memset(plane[:].rearrange("p e i -> p (e i)").bitcast(I32), 0)
         make_identity(nc, ident0[:])
         nc.scalar.activation(ident[:], ident0[:], ACT.Relu)
 
-        load_token_plane(xs, x_scales)
+        for q in range(4):
+            load_token_rows(q, nc.sync if q < 2 else nc.scalar)
         load_words(xw, x_words)
         nc.sync.dma_start(offs_t[:], offs)
-        load_expert_words(w1w[0], w1_words, 0, 2)
-        load_planes(w1c, w1_scales[:, 0])
-        for g in range(1, PAIRS):
-            load_expert_words(w1w[g], w1_words, 2 * g, 2 * g + 2)
-        load_planes(w1sc, w1s_scales)
+        load_expert_words(w1w[0], w1_words, *W1_LOADS[0])
+        load_planes(w1c[0], w1_scales[0:4, 0])
+        load_expert_words(w1w[1], w1_words, *W1_LOADS[1])
+        load_expert_words(w1w[2], w1_words, *W1_LOADS[2])
+        load_planes(w1c[1], w1_scales[4:E, 0])
+        load_expert_words(w1w[3], w1_words, *W1_LOADS[3])
+        load_planes(w1sc, w1s_scales, nc.gpsimd)
         load_words(w1sw, w1s_words)
         load_planes(w2c, w2_scales[:, 0])
         load_expert_words(w2w, w2_words, 0, E)
@@ -103,27 +109,32 @@ def tile_moe_shf_mlp_relu2_kernel(
         load_planes(w2sc, w2s_scales)
         load_words(w2sw, w2s_words)
 
-        pre, rect, turned, acc, picked, ys, ys_sb, zsum, summed, back, result = ({} for k in range(11))
+        pre, rect, turned, acc, picked, gated, part, ys, ys_sb, zsum, summed, back, result = ({} for k in range(13))
 
         def gather_tokens(g):
-            lst = offs_t[:, 16 * g : 16 * (g + 1)]
+            e0, e1 = GATHERS[g]
+            lst = offs_t[:, e0 * C // 16 : e1 * C // 16]
             nc.vector.tensor_copy(xgw[g][:], xw[:].bitcast(U32).indirect(lst))
             nc.vector.tensor_copy(xgs[g][:], xs[:].indirect(lst))
 
         def layer1(u, b):
             pre[u] = bank(b, [P, H])
-            if u < E:
-                cols = slice(C * (u % 2), C * (u % 2 + 1))
-                nc.tensor.matmul_mx(
-                    out=pre[u][:], lhsT=xgw[u // 2][:, cols].bitcast(FP8X4), lhsT_scale=xgs[u // 2][:, cols],
-                    rhs=w1w[u // 2][:, u % 2, :].bitcast(FP4X4), rhs_scale=w1c[:, u, :], start=True, stop=True,
-                )
-            else:
-                cols = slice(C * (u - E), C * (u - E + 1))
-                nc.tensor.matmul_mx(
-                    out=pre[u][:], lhsT=xw[:, cols].bitcast(FP8X4), lhsT_scale=xs[:, cols],
-                    rhs=w1sw[:].bitcast(FP8X4), rhs_scale=w1sc[:, 0, :], start=True, stop=True,
-                )
+            g, k = place(GATHERS, u)
+            w, j = place(W1_LOADS, u)
+            c, i = place(W1_PLANES, u)
+            cols = slice(C * k, C * (k + 1))
+            nc.tensor.matmul_mx(
+                out=pre[u][:], lhsT=xgw[g][:, cols].bitcast(FP8X4), lhsT_scale=xgs[g][:, cols],
+                rhs=w1w[w][:, j, :].bitcast(FP4X4), rhs_scale=w1c[c][:, i, :], start=True, stop=True,
+            )
+
+        def shared1(u, b):
+            pre[u] = bank(b, [P, H])
+            cols = slice(C * (u - E), C * (u - E + 1))
+            nc.tensor.matmul_mx(
+                out=pre[u][:], lhsT=xw[:, cols].bitcast(FP8X4), lhsT_scale=xs[:, cols],
+                rhs=w1sw[:].bitcast(FP8X4), rhs_scale=w1sc[:, 0, :], start=True, stop=True,
+            )
 
         def rectify(u, tag=""):
             rect[u] = held("rect%d" % u, [P, 4, P], F32, tag)
@@ -139,55 +150,73 @@ def tile_moe_shf_mlp_relu2_kernel(
                 nc.tensor.transpose(turned[u][:, t, :], rect[u][:, t, :], ident[:])
 
         def square(u):
-            g, k = (u // 2, u % 2) if u < E else (PAIRS, u - E)
-            nc.scalar.activation(hb[g][:, C * k : C * (k + 1), :], turned[u][:].rearrange("p t s -> p s t"), ACT.Square)
+            g, k = place(HIDDEN, u)
+            dst = hb[g][:, C * k : C * (k + 1), :]
+            nc.scalar.activation(dst, turned[u][:].rearrange("p t s -> p s t"), ACT.Square)
 
-        def quantise(g, c0=0, c1=None):
+        def quantise(u0, u1, tag=""):
+            g, k = place(HIDDEN, u0)
+            if g not in hw:
+                hw[g] = held("hw%d" % HIDDEN[g][0], [P, (HIDDEN[g][1] - HIDDEN[g][0]) * C], U32, tag)
+            cols = slice(C * k, C * (k + u1 - u0))
             nc.vector.quantize_mx(
-                out=hw[g][:, c0:c1].bitcast(FP8X4), scales=hc[g][:, c0:c1], in_=hb[g][:, c0:c1, :].rearrange("p s t -> p (s t)")
+                out=hw[g][:, cols].bitcast(FP8X4), scales=hc[g][:, cols], in_=hb[g][:, cols, :].rearrange("p s t -> p (s t)")
             )
 
         def layer2(j, e0, e1, b):
             acc[j, e0] = bank(b, [P, (e1 - e0) * C])
             for e in range(e0, e1):
-                cols = slice(C * (e % 2), C * (e % 2 + 1))
+                g, k = place(HIDDEN, e)
+                cols = slice(C * k, C * (k + 1))
                 nc.tensor.matmul_mx(
                     out=acc[j, e0][:, C * (e - e0) : C * (e - e0 + 1)],
                     lhsT=w2w[:, e, 2 * P * j : 2 * P * (j + 1)].bitcast(FP4X4), lhsT_scale=w2c[:, e, P * j : P * (j + 1)],
-                    rhs=hw[e // 2][:, cols].bitcast(FP8X4), rhs_scale=hc[e // 2][:, cols], start=True, stop=True,
+                    rhs=hw[g][:, cols].bitcast(FP8X4), rhs_scale=hc[g][:, cols], start=True, stop=True,
                 )
 
-        def drain(j, e0, copy=nc.scalar.copy):
+        def drain(j, e0, copy=nc.scalar.copy, tag=""):
+            if j not in y:
+                y[j] = held("y%d" % j, [P, S], F32, tag)
             copy(y[j][:, C * e0 : C * e0 + acc[j, e0].shape[1]], acc[j, e0][:])
 
         def pick(j, r, t0=0, t1=T, tag=""):
-            picked[j, r, t0] = held("picked%d_%d_%d" % (j, r, t0), [P, t1 - t0], F32, tag)
+            gated[j, r, t0] = held("picked%d_%d_%d" % (j, r, t0), [P, t1 - t0], F32, tag)
             nc.vector.tensor_tensor(
-                picked[j, r, t0][:], y[j][:].indirect(pos_t[r][:, t0 // 16 : t1 // 16]), gate_t[:, r, t0:t1], ALU.mult
+                gated[j, r, t0][:], y[j][:].indirect(pos_t[r][:, t0 // 16 : t1 // 16]), gate_t[:, r, t0:t1], ALU.mult
+            )
+
+        def fetch(j, r, t0=0, t1=T, tag=""):
+            picked[j, r, t0] = held("fetched%d_%d_%d" % (j, r, t0), [P, t1 - t0], F32, tag)
+            nc.scalar.activation(picked[j, r, t0][:], y[j][:].indirect(pos_t[r][:, t0 // 16 : t1 // 16]), ACT.Copy)
+
+        def weigh(j, r, t0=0, t1=T, base=0, tag=""):
+            gated[j, r, t0] = held("gated%d_%d_%d" % (j, r, t0), [P, t1 - t0], F32, tag)
+            nc.vector.tensor_tensor(
+                gated[j, r, t0][:], picked[j, r, base][:, t0 - base : t1 - base], gate_t[:, r, t0:t1], ALU.mult
             )
 
         def shared_rows(j, b):
             ys[j] = bank(b, [P, T])
+            g = len(HIDDEN) - 1
             nc.tensor.matmul_mx(
                 out=ys[j][:], lhsT=w2sw[:, P * j : P * (j + 1)].bitcast(FP8X4), lhsT_scale=w2sc[:, 0, P * j : P * (j + 1)],
-                rhs=hw[PAIRS][:].bitcast(FP8X4), rhs_scale=hc[PAIRS][:], start=True, stop=True,
+                rhs=hw[g][:].bitcast(FP8X4), rhs_scale=hc[g][:], start=True, stop=True,
             )
 
-        def park(j):
-            ys_sb[j] = held("ys_sb%d" % j, [P, T], F32)
+        def park(j, tag=""):
+            ys_sb[j] = held("ys_sb%d" % j, [P, T], F32, tag)
             nc.scalar.copy(ys_sb[j][:], ys[j][:])
 
-        def add_turned(j, term, first, last):
+        def add_turned(j, term, first=False, last=False):
             for tb in range(4):
                 nc.tensor.matmul(
                     zsum[j][:, tb, :], term[:, P * tb : P * (tb + 1)], ident[:],
                     start=(first and tb == 0), stop=(last and tb == 3), is_transpose=True,
                 )
 
-        def add_routed(j, b):
+        def open_sum(j, b, term):
             zsum[j] = bank(b, [P, 4, P])
-            add_turned(j, picked[j, 0, 0], True, False)
-            add_turned(j, picked[j, 1, 0], False, False)
+            add_turned(j, term, first=True)
 
         def drain_sum(j, tag=""):
             summed[j] = held("summed%d" % j, [P, 4, P], F32, tag)
@@ -198,20 +227,33 @@ def tile_moe_shf_mlp_relu2_kernel(
             for tb in range(4):
                 nc.tensor.transpose(back[j][:, tb, :], summed[j][:, tb, :], ident[:])
 
-        def drain_back(j):
-            result[j] = held("res%d" % j, [P, T], F32)
+        def drain_back(j, tag=""):
+            result[j] = held("res%d" % j, [P, T], F32, tag)
             nc.scalar.copy(result[j][:], back[j][:].rearrange("p a b -> p (a b)"))
 
         def store(j, queue):
             queue.dma_start(out[P * j : P * (j + 1), :], result[j][:])
 
-        idle = bank(7, [P, T])
-        for k in range(3):
-            nc.tensor.matmul_mx(
-                out=idle[:], lhsT=xw[:, 0:P].bitcast(FP8X4), lhsT_scale=xs[:, 0:P],
-                rhs=xw[:].bitcast(FP8X4), rhs_scale=xs[:], start=True, stop=True,
-            )
-        for g in range(PAIRS):
+        def add_shared(j, r, tag=""):
+            part[j] = held("part%d" % j, [P, T], F32, tag)
+            nc.vector.tensor_tensor(part[j][:], gated[j, r, 0][:], ys[j][:], ALU.add)
+
+        def finish(j, r, t0=0, t1=T, base=None, tag=""):
+            base = t0 if base is None else base
+            res = held("res%d_%d" % (j, t0), [P, t1 - t0], F32, tag)
+            nc.vector.tensor_tensor(res[:], part[j][:, t0:t1], gated[j, r, base][:, t0 - base : t1 - base], ALU.add)
+            nc.sync.dma_start(out[P * j : P * (j + 1), t0:t1], res[:])
+
+        def warm(b, passes):
+            idle = bank(b, [P, T])
+            for k in range(passes):
+                nc.tensor.matmul_mx(
+                    out=idle[:], lhsT=xw[:, 0:P].bitcast(FP8X4), lhsT_scale=xs[:, 0:P],
+                    rhs=xw[:].bitcast(FP8X4), rhs_scale=xs[:], start=True, stop=True,
+                )
+
+        warm(7, 2)
+        for g in range(len(GATHERS)):
             gather_tokens(g)
         for u in range(4):
             layer1(u, u)
@@ -232,29 +274,30 @@ def tile_moe_shf_mlp_relu2_kernel(
             rectify(u)
         turn(4, 7)
         turn(5, 0)
-        layer1(8, 1)
-        layer1(9, 2)
+        shared1(8, 1)
+        shared1(9, 2)
         turn(6, 5)
         turn(7, 6)
-        layer1(10, 3)
-        layer1(11, 4)
+        shared1(10, 3)
+        shared1(11, 4)
         for u in range(4, 8):
             square(u)
-        quantise(0)
-        quantise(1)
+        quantise(0, 2)
+        quantise(2, 4)
         rectify(8)
-        quantise(2)
-        quantise(3, 0, C)
+        quantise(4, 6)
+        quantise(6, 7)
         rectify(9)
-        quantise(3, C, 2 * C)
+        quantise(7, 8)
         rectify(10)
-        rectify(11, "hb3")
+        rectify(11, "hb6")
         layer2(0, 0, 4, 7)
         layer2(0, 4, 7, 0)
         layer2(0, 7, 8, 1)
         drain(0, 0)
         drain(0, 4)
         drain(0, 7, nc.vector.tensor_copy)
+
         layer2(1, 0, 4, 5)
         layer2(1, 4, 8, 6)
         drain(1, 0)
@@ -265,32 +308,33 @@ def tile_moe_shf_mlp_relu2_kernel(
         for u, b in zip(range(E, UNITS), (7, 0, 5, 6)):
             turn(u, b)
             square(u)
-        quantise(PAIRS)
+        quantise(8, 12)
         layer2(2, 0, 4, 7)
         layer2(2, 4, 8, 0)
         layer2(3, 0, 4, 5)
         layer2(3, 4, 8, 6)
-        pick(1, 1, tag="hw2")
+        pick(1, 1, tag="hw4")
         for j in (2, 3):
             drain(j, 0)
             drain(j, 4)
-        add_routed(0, 7)
+        open_sum(0, 7, gated[0, 0, 0])
+        add_turned(0, gated[0, 1, 0])
         for j, b in enumerate((1, 2, 3, 4)):
             shared_rows(j, b)
         pick(2, 0)
         pick(2, 1)
         park(0)
         park(1)
-        add_turned(0, ys_sb[0], False, True)
-        add_routed(1, 0)
-        add_turned(1, ys_sb[1], False, True)
+        add_turned(0, ys_sb[0], last=True)
+        open_sum(1, 0, gated[1, 0, 0])
+        add_turned(1, gated[1, 1, 0])
+        add_turned(1, ys_sb[1], last=True)
         park(2)
-        zsum[2] = bank(2, [P, 4, P])
-        add_turned(2, picked[2, 0, 0], True, False)
-        add_turned(2, ys_sb[2], False, False)
+        open_sum(2, 2, gated[2, 0, 0])
+        add_turned(2, ys_sb[2])
         drain_sum(0, "summed_a")
         turn_back(0, 5)
-        add_turned(2, picked[2, 1, 0], False, True)
+        add_turned(2, gated[2, 1, 0], last=True)
         drain_sum(1)
         turn_back(1, 6)
         drain_back(0)
@@ -301,15 +345,10 @@ def tile_moe_shf_mlp_relu2_kernel(
         store(1, nc.scalar)
         drain_back(2)
         store(2, nc.scalar)
-
-        j = NT - 1
         cut = T - LAST_PIECE
-        part = held("part", [P, T], F32)
-        pick(j, 0)
-        pick(j, 1, 0, cut)
-        nc.vector.tensor_tensor(part[:], picked[j, 0, 0][:], ys[j][:], ALU.add)
-        pick(j, 1, cut, T)
-        for t0, t1 in ((0, cut), (cut, T)):
-            res = held("res3_%d" % t0, [P, t1 - t0], F32)
-            nc.vector.tensor_tensor(res[:], part[:, t0:t1], picked[j, 1, t0][:], ALU.add)
-            nc.sync.dma_start(out[P * j : P * (j + 1), t0:t1], res[:])
+        pick(3, 0)
+        pick(3, 1, 0, cut)
+        add_shared(3, 0)
+        pick(3, 1, cut, T)
+        finish(3, 1, 0, cut)
+        finish(3, 1, cut, T)

@@ -25,7 +25,8 @@ NT = N // P
 GATHERS = ((0, 2), (2, 4), (4, 6), (6, 8))
 W1_LOADS = ((0, 2), (2, 4), (4, 6), (6, 8))
 W1_PLANES = ((0, 4), (4, 8))
-HIDDEN = ((0, 2), (2, 4), (4, 6), (6, 8), (8, 12))
+W2_LOADS = ((0, 8),)
+HIDDEN = ((0, 4), (4, 6), (6, 8), (8, 12))
 RELU_ON_VECTOR = (4, 5, 6, 7, 8, 9, 11)
 LAST_PIECE = 128
 
@@ -53,7 +54,7 @@ def tile_moe_shf_mlp_relu2_kernel(
         xgs = [held("xgs%d" % e0, [P, (e1 - e0) * C], U8) for e0, e1 in GATHERS]
         w1w = [held("w1w%d" % e0, [P, e1 - e0, 2 * H], U8) for e0, e1 in W1_LOADS]
         w1c = [held("w1c%d" % e0, [P, e1 - e0, H], U8) for e0, e1 in W1_PLANES]
-        w2w = held("w2w", [P, E, 2 * N], U8)
+        w2w = [held("w2w%d" % e0, [P, e1 - e0, 2 * N], U8) for e0, e1 in W2_LOADS]
         w2c = held("w2c", [P, E, N], U8)
         w1sw = held("w1sw", [P, HS], I32)
         w1sc = held("w1sc", [P, 1, HS], U8)
@@ -77,37 +78,37 @@ def tile_moe_shf_mlp_relu2_kernel(
             rows = x_scales[0, 4 * q : 4 * q + 4, :].bitcast(I32)
             queue.dma_start(xs[32 * q : 32 * (q + 1), :].bitcast(I32), rows.unsqueeze(0).to_broadcast([8, 4, rows.shape[1]]))
 
-        def load_planes(dst, src, queue=nc.sync):
-            for r in range(4):
+        def load_planes(dst, src, queues=(nc.sync,) * 4):
+            for r, queue in enumerate(queues):
                 queue.dma_start(dst[r:P:32, :, :].bitcast(I32), src[:, r:16:4, :].rearrange("e b i -> b e i").bitcast(I32))
 
-        def load_expert_words(dst, src, e0, e1):
-            nc.sync.dma_start(dst[:].bitcast(I32), src[e0:e1, 0].rearrange("e p c -> p e c").bitcast(I32))
+        def load_expert_words(dst, src, e0, e1, queue=nc.sync):
+            queue.dma_start(dst[:].bitcast(I32), src[e0:e1, 0].rearrange("e p c -> p e c").bitcast(I32))
 
         for plane in (w1c[0], w1sc, w1c[1], w2c, w2sc):
             nc.vector.memset(plane[:].rearrange("p e i -> p (e i)").bitcast(I32), 0)
-        make_identity(nc, ident0[:])
-        nc.scalar.activation(ident[:], ident0[:], ACT.Relu)
-
         for q in range(4):
             load_token_rows(q, nc.sync if q < 2 else nc.scalar)
         load_words(xw, x_words)
         nc.sync.dma_start(offs_t[:], offs)
         load_expert_words(w1w[0], w1_words, *W1_LOADS[0])
-        load_planes(w1c[0], w1_scales[0:4, 0])
+        load_planes(w1c[0], w1_scales[0:4, 0], (nc.sync,) * 4)
+        make_identity(nc, ident0[:])
         load_expert_words(w1w[1], w1_words, *W1_LOADS[1])
-        load_expert_words(w1w[2], w1_words, *W1_LOADS[2])
         load_planes(w1c[1], w1_scales[4:E, 0])
+        load_expert_words(w1w[2], w1_words, *W1_LOADS[2])
         load_expert_words(w1w[3], w1_words, *W1_LOADS[3])
-        load_planes(w1sc, w1s_scales, nc.gpsimd)
+        load_planes(w1sc, w1s_scales, (nc.gpsimd,) * 4)
         load_words(w1sw, w1s_words)
         load_planes(w2c, w2_scales[:, 0])
-        load_expert_words(w2w, w2_words, 0, E)
+        for half, (e0, e1) in zip(w2w, W2_LOADS):
+            load_expert_words(half, w2_words, e0, e1)
         for r, pos in enumerate((pos1, pos2)):
             nc.sync.dma_start(pos_t[r][:], pos)
         nc.sync.dma_start(gate_t[:], gate.rearrange("r p t -> p r t"))
         load_planes(w2sc, w2s_scales)
         load_words(w2sw, w2s_words)
+        nc.scalar.activation(ident[:], ident0[:], ACT.Relu)
 
         pre, rect, turned, acc, picked, gated, part, ys, ys_sb, zsum, summed, back, result = ({} for k in range(13))
 
@@ -167,10 +168,11 @@ def tile_moe_shf_mlp_relu2_kernel(
             acc[j, e0] = bank(b, [P, (e1 - e0) * C])
             for e in range(e0, e1):
                 g, k = place(HIDDEN, e)
+                w, i = place(W2_LOADS, e)
                 cols = slice(C * k, C * (k + 1))
                 nc.tensor.matmul_mx(
                     out=acc[j, e0][:, C * (e - e0) : C * (e - e0 + 1)],
-                    lhsT=w2w[:, e, 2 * P * j : 2 * P * (j + 1)].bitcast(FP4X4), lhsT_scale=w2c[:, e, P * j : P * (j + 1)],
+                    lhsT=w2w[w][:, i, 2 * P * j : 2 * P * (j + 1)].bitcast(FP4X4), lhsT_scale=w2c[:, e, P * j : P * (j + 1)],
                     rhs=hw[g][:, cols].bitcast(FP8X4), rhs_scale=hc[g][:, cols], start=True, stop=True,
                 )
 
@@ -218,21 +220,22 @@ def tile_moe_shf_mlp_relu2_kernel(
             zsum[j] = bank(b, [P, 4, P])
             add_turned(j, term, first=True)
 
-        def drain_sum(j, tag=""):
-            summed[j] = held("summed%d" % j, [P, 4, P], F32, tag)
-            nc.scalar.copy(summed[j][:], zsum[j][:])
+        def drain_sum(j, tag="", b0=0, b1=4):
+            summed[j, b0] = held("summed%d_%d" % (j, b0), [P, b1 - b0, P], F32, tag)
+            nc.scalar.copy(summed[j, b0][:], zsum[j][:, b0:b1, :])
 
-        def turn_back(j, b):
-            back[j] = bank(b, [P, 4, P])
-            for tb in range(4):
-                nc.tensor.transpose(back[j][:, tb, :], summed[j][:, tb, :], ident[:])
+        def turn_back(j, b, b0=0):
+            back[j, b0] = bank(b, summed[j, b0].shape)
+            for tb in range(summed[j, b0].shape[1]):
+                nc.tensor.transpose(back[j, b0][:, tb, :], summed[j, b0][:, tb, :], ident[:])
 
-        def drain_back(j, tag=""):
-            result[j] = held("res%d" % j, [P, T], F32, tag)
-            nc.scalar.copy(result[j][:], back[j][:].rearrange("p a b -> p (a b)"))
+        def drain_back(j, b0=0):
+            result[j, b0] = held("res%d_%d" % (j, b0), back[j, b0].shape, F32)
+            nc.scalar.copy(result[j, b0][:], back[j, b0][:])
 
-        def store(j, queue):
-            queue.dma_start(out[P * j : P * (j + 1), :], result[j][:])
+        def store(j, queue, b0=0):
+            rows = result[j, b0][:].rearrange("p a b -> p (a b)")
+            queue.dma_start(out[P * j : P * (j + 1), P * b0 : P * b0 + rows.shape[1]], rows)
 
         def add_shared(j, r, tag=""):
             part[j] = held("part%d" % j, [P, T], F32, tag)
@@ -240,7 +243,7 @@ def tile_moe_shf_mlp_relu2_kernel(
 
         def finish(j, r, t0=0, t1=T, base=None, tag=""):
             base = t0 if base is None else base
-            res = held("res%d_%d" % (j, t0), [P, t1 - t0], F32, tag)
+            res = held("last%d_%d" % (j, t0), [P, t1 - t0], F32, tag)
             nc.vector.tensor_tensor(res[:], part[j][:, t0:t1], gated[j, r, base][:, t0 - base : t1 - base], ALU.add)
             nc.sync.dma_start(out[P * j : P * (j + 1), t0:t1], res[:])
 
@@ -260,91 +263,97 @@ def tile_moe_shf_mlp_relu2_kernel(
         for u in range(4):
             rectify(u)
         turn(0, 4)
-        turn(1, 0)
-        layer1(4, 1)
-        layer1(5, 2)
-        turn(2, 5)
-        turn(3, 6)
-        layer1(6, 3)
-        square(0)
-        layer1(7, 4)
-        for u in range(1, 4):
+        layer1(4, 0)
+        layer1(5, 1)
+        turn(1, 6)
+        turn(2, 7)
+        turn(3, 5)
+        layer1(6, 2)
+        layer1(7, 3)
+        rectify(4)
+        rectify(5)
+        turn(4, 0)
+        turn(5, 1)
+        for u in range(4):
             square(u)
-        for u in range(4, 8):
-            rectify(u)
-        turn(4, 7)
-        turn(5, 0)
-        shared1(8, 1)
-        shared1(9, 2)
-        turn(6, 5)
-        turn(7, 6)
-        shared1(10, 3)
-        shared1(11, 4)
-        for u in range(4, 8):
-            square(u)
-        quantise(0, 2)
-        quantise(2, 4)
+        rectify(6)
+        rectify(7)
+        shared1(8, 7)
+        turn(6, 6)
+        turn(7, 2)
+        shared1(9, 3)
+        square(4)
+        square(5)
+        shared1(10, 1)
+        square(6)
+        square(7)
+        quantise(0, 4)
+        layer2(0, 0, 4, 0)
+        shared1(11, 6)
         rectify(8)
         quantise(4, 6)
         quantise(6, 7)
         rectify(9)
         quantise(7, 8)
         rectify(10)
-        rectify(11, "hb6")
-        layer2(0, 0, 4, 7)
-        layer2(0, 4, 7, 0)
-        layer2(0, 7, 8, 1)
+        rectify(11)
+        layer2(0, 4, 7, 2)
+        layer2(0, 7, 8, 4)
         drain(0, 0)
         drain(0, 4)
         drain(0, 7, nc.vector.tensor_copy)
 
-        layer2(1, 0, 4, 5)
+        layer2(1, 0, 4, 1)
         layer2(1, 4, 8, 6)
         drain(1, 0)
         drain(1, 4)
         pick(0, 0)
         pick(0, 1)
         pick(1, 0)
-        for u, b in zip(range(E, UNITS), (7, 0, 5, 6)):
+        for u, b in zip(range(E, UNITS), (0, 2, 1, 6)):
             turn(u, b)
             square(u)
         quantise(8, 12)
-        layer2(2, 0, 4, 7)
-        layer2(2, 4, 8, 0)
-        layer2(3, 0, 4, 5)
+        layer2(2, 0, 4, 0)
+        layer2(2, 4, 8, 2)
+        layer2(3, 0, 4, 1)
         layer2(3, 4, 8, 6)
         pick(1, 1, tag="hw4")
         for j in (2, 3):
             drain(j, 0)
             drain(j, 4)
-        open_sum(0, 7, gated[0, 0, 0])
+        open_sum(0, 0, gated[0, 0, 0])
         add_turned(0, gated[0, 1, 0])
-        for j, b in enumerate((1, 2, 3, 4)):
+        for j, b in enumerate((4, 5, 7, 3)):
             shared_rows(j, b)
         pick(2, 0)
         pick(2, 1)
         park(0)
         park(1)
         add_turned(0, ys_sb[0], last=True)
-        open_sum(1, 0, gated[1, 0, 0])
+        open_sum(1, 2, gated[1, 0, 0])
         add_turned(1, gated[1, 1, 0])
         add_turned(1, ys_sb[1], last=True)
         park(2)
-        open_sum(2, 2, gated[2, 0, 0])
+        open_sum(2, 5, gated[2, 0, 0])
         add_turned(2, ys_sb[2])
         drain_sum(0, "summed_a")
-        turn_back(0, 5)
+        turn_back(0, 1)
         add_turned(2, gated[2, 1, 0], last=True)
         drain_sum(1)
         turn_back(1, 6)
         drain_back(0)
-        drain_sum(2, "summed_a")
-        turn_back(2, 1)
-        drain_back(1)
+        drain_sum(2, "summed_a", 0, 2)
         store(0, nc.scalar)
+        drain_sum(2, "", 2, 4)
+        turn_back(2, 4, 0)
+        turn_back(2, 7, 2)
+        drain_back(1)
+        drain_back(2, 0)
         store(1, nc.scalar)
-        drain_back(2)
-        store(2, nc.scalar)
+        drain_back(2, 2)
+        store(2, nc.scalar, 0)
+        store(2, nc.scalar, 2)
         cut = T - LAST_PIECE
         pick(3, 0)
         pick(3, 1, 0, cut)

@@ -100,9 +100,9 @@ def tile_moe_shf_mlp_relu2_kernel(
         load_expert_words(w1w[3], w1_words, *W1_LOADS[3])
         load_planes(w1sc, w1s_scales, (nc.gpsimd,) * 4)
         load_words(w1sw, w1s_words)
-        load_planes(w2c, w2_scales[:, 0])
         for half, (e0, e1) in zip(w2w, W2_LOADS):
             load_expert_words(half, w2_words, e0, e1)
+        load_planes(w2c, w2_scales[:, 0])
         for r, pos in enumerate((pos1, pos2)):
             nc.sync.dma_start(pos_t[r][:], pos)
         nc.sync.dma_start(gate_t[:], gate.rearrange("r p t -> p r t"))
@@ -285,11 +285,11 @@ def tile_moe_shf_mlp_relu2_kernel(
         square(4)
         square(5)
         shared1(10, 1)
+        shared1(11, 0)
         square(6)
         square(7)
         quantise(0, 4)
-        layer2(0, 0, 4, 0)
-        shared1(11, 6)
+        layer2(0, 0, 4, 6)
         rectify(8)
         quantise(4, 6)
         quantise(6, 7)
@@ -304,25 +304,25 @@ def tile_moe_shf_mlp_relu2_kernel(
         drain(0, 7, nc.vector.tensor_copy)
 
         layer2(1, 0, 4, 1)
-        layer2(1, 4, 8, 6)
+        layer2(1, 4, 8, 0)
         drain(1, 0)
         drain(1, 4)
         pick(0, 0)
         pick(0, 1)
         pick(1, 0)
-        for u, b in zip(range(E, UNITS), (0, 2, 1, 6)):
+        for u, b in zip(range(E, UNITS), (6, 2, 1, 0)):
             turn(u, b)
             square(u)
         quantise(8, 12)
-        layer2(2, 0, 4, 0)
+        layer2(2, 0, 4, 6)
         layer2(2, 4, 8, 2)
         layer2(3, 0, 4, 1)
-        layer2(3, 4, 8, 6)
+        layer2(3, 4, 8, 0)
         pick(1, 1, tag="hw4")
         for j in (2, 3):
             drain(j, 0)
             drain(j, 4)
-        open_sum(0, 0, gated[0, 0, 0])
+        open_sum(0, 6, gated[0, 0, 0])
         add_turned(0, gated[0, 1, 0])
         for j, b in enumerate((4, 5, 7, 3)):
             shared_rows(j, b)
@@ -341,7 +341,7 @@ def tile_moe_shf_mlp_relu2_kernel(
         turn_back(0, 1)
         add_turned(2, gated[2, 1, 0], last=True)
         drain_sum(1)
-        turn_back(1, 6)
+        turn_back(1, 0)
         drain_back(0)
         drain_sum(2, "summed_a", 0, 2)
         store(0, nc.scalar)

@@ -25,7 +25,7 @@ NT = N // P
 GATHERS = ((0, 2), (2, 4), (4, 6), (6, 8))
 W1_LOADS = ((0, 2), (2, 4), (4, 6), (6, 8))
 W1_PLANES = ((0, 4), (4, 8))
-W2_LOADS = ((0, 8),)
+W2_LOADS = ((0, 2), (2, 4))
 HIDDEN = ((0, 4), (4, 6), (6, 8), (8, 12))
 RELU_ON_VECTOR = (4, 5, 6, 7, 8, 9, 11)
 LAST_PIECE = 128
@@ -54,7 +54,7 @@ def tile_moe_shf_mlp_relu2_kernel(
         xgs = [held("xgs%d" % e0, [P, (e1 - e0) * C], U8) for e0, e1 in GATHERS]
         w1w = [held("w1w%d" % e0, [P, e1 - e0, 2 * H], U8) for e0, e1 in W1_LOADS]
         w1c = [held("w1c%d" % e0, [P, e1 - e0, H], U8) for e0, e1 in W1_PLANES]
-        w2w = [held("w2w%d" % e0, [P, e1 - e0, 2 * N], U8) for e0, e1 in W2_LOADS]
+        w2w = [held("w2w%d" % j0, [P, E, 2 * P * (j1 - j0)], U8) for j0, j1 in W2_LOADS]
         w2c = held("w2c", [P, E, N], U8)
         w1sw = held("w1sw", [P, HS], I32)
         w1sc = held("w1sc", [P, 1, HS], U8)
@@ -82,6 +82,11 @@ def tile_moe_shf_mlp_relu2_kernel(
             for r, queue in enumerate(queues):
                 queue.dma_start(dst[r:P:32, :, :].bitcast(I32), src[:, r:16:4, :].rearrange("e b i -> b e i").bitcast(I32))
 
+        def load_w2_rows(g):
+            j0, j1 = W2_LOADS[g]
+            src = w2_words[:, 0, :, 2 * P * j0 : 2 * P * j1].rearrange("e p c -> p e c")
+            nc.sync.dma_start(w2w[g][:].bitcast(I32), src.bitcast(I32))
+
         def load_expert_words(dst, src, e0, e1, queue=nc.sync):
             queue.dma_start(dst[:].bitcast(I32), src[e0:e1, 0].rearrange("e p c -> p e c").bitcast(I32))
 
@@ -100,12 +105,12 @@ def tile_moe_shf_mlp_relu2_kernel(
         load_expert_words(w1w[3], w1_words, *W1_LOADS[3])
         load_planes(w1sc, w1s_scales, (nc.gpsimd,) * 4)
         load_words(w1sw, w1s_words)
-        for half, (e0, e1) in zip(w2w, W2_LOADS):
-            load_expert_words(half, w2_words, e0, e1)
+        load_w2_rows(0)
         load_planes(w2c, w2_scales[:, 0])
         for r, pos in enumerate((pos1, pos2)):
             nc.sync.dma_start(pos_t[r][:], pos)
         nc.sync.dma_start(gate_t[:], gate.rearrange("r p t -> p r t"))
+        load_w2_rows(1)
         load_planes(w2sc, w2s_scales)
         load_words(w2sw, w2s_words)
         nc.scalar.activation(ident[:], ident0[:], ACT.Relu)
@@ -168,13 +173,30 @@ def tile_moe_shf_mlp_relu2_kernel(
             acc[j, e0] = bank(b, [P, (e1 - e0) * C])
             for e in range(e0, e1):
                 g, k = place(HIDDEN, e)
-                w, i = place(W2_LOADS, e)
+                w, i = place(W2_LOADS, j)
                 cols = slice(C * k, C * (k + 1))
                 nc.tensor.matmul_mx(
                     out=acc[j, e0][:, C * (e - e0) : C * (e - e0 + 1)],
-                    lhsT=w2w[w][:, i, 2 * P * j : 2 * P * (j + 1)].bitcast(FP4X4), lhsT_scale=w2c[:, e, P * j : P * (j + 1)],
+                    lhsT=w2w[w][:, e, 2 * P * i : 2 * P * (i + 1)].bitcast(FP4X4), lhsT_scale=w2c[:, e, P * j : P * (j + 1)],
                     rhs=hw[g][:, cols].bitcast(FP8X4), rhs_scale=hc[g][:, cols], start=True, stop=True,
                 )
+
+        def layer2_mixed(j, g, b):
+            acc[j, g] = bank(b, [P, 2, 2 * C])
+            for e in (2 * g, 2 * g + 1, 2 * g + 4, 2 * g + 5):
+                h, k = place(HIDDEN, e)
+                w, i = place(W2_LOADS, j)
+                cols = slice(C * k, C * (k + 1))
+                nc.tensor.matmul_mx(
+                    out=acc[j, g][:, e // 4, C * (e % 2) : C * (e % 2 + 1)],
+                    lhsT=w2w[w][:, e, 2 * P * i : 2 * P * (i + 1)].bitcast(FP4X4), lhsT_scale=w2c[:, e, P * j : P * (j + 1)],
+                    rhs=hw[h][:, cols].bitcast(FP8X4), rhs_scale=hc[h][:, cols], start=True, stop=True,
+                )
+
+        def drain_mixed(j, g):
+            if j not in y:
+                y[j] = held("y%d" % j, [P, S], F32)
+            nc.scalar.copy(y[j][:].rearrange("p (h g c) -> p g h c", h=2, g=2)[:, g], acc[j, g][:])
 
         def drain(j, e0, copy=nc.scalar.copy, tag=""):
             if j not in y:

@@ -269,15 +269,6 @@ def tile_moe_shf_mlp_relu2_kernel(
             nc.vector.tensor_tensor(res[:], part[j][:, t0:t1], gated[j, r, base][:, t0 - base : t1 - base], ALU.add)
             nc.sync.dma_start(out[P * j : P * (j + 1), t0:t1], res[:])
 
-        def warm(b, passes):
-            idle = bank(b, [P, T])
-            for k in range(passes):
-                nc.tensor.matmul_mx(
-                    out=idle[:], lhsT=xw[:, 0:P].bitcast(FP8X4), lhsT_scale=xs[:, 0:P],
-                    rhs=xw[:].bitcast(FP8X4), rhs_scale=xs[:], start=True, stop=True,
-                )
-
-        warm(7, 2)
         for g in range(len(GATHERS)):
             gather_tokens(g)
         for u in range(4):

from contextlib import ExitStack

import concourse.mybir as mybir
from concourse.masks import make_identity

K, T, E, C, H, HS, N = 512, 512, 8, 128, 512, 512, 512
S = E * C
FLOPS = 2 * K * H * S + 2 * H * N * S + 2 * K * HS * T + 2 * HS * N * T

F32 = mybir.dt.float32
BF16 = mybir.dt.bfloat16
I32 = mybir.dt.int32
U32 = mybir.dt.uint32
U16 = mybir.dt.uint16
U8 = mybir.dt.uint8
FP8X4 = mybir.dt.float8_e4m3fn_x4
FP4X4 = mybir.dt.float4_e2m1fn_x4
ACT = mybir.ActivationFunctionType
ALU = mybir.AluOpType

P = 128
PAIRS = E // 2
UNITS = E + T // C
NT = N // P
GATHERS = ((0, 2), (2, 4), (4, 6), (6, 8))
W1_LOADS = ((0, 2), (2, 4), (4, 6), (6, 8))
W1_PLANES = ((0, 4), (4, 8))
W2_LOADS = ((0, 2), (2, 4))
HIDDEN = ((0, 4), (4, 6), (6, 8), (8, 12))
RELU_ON_VECTOR = (4, 5, 6, 7, 8, 9, 11)
LAST_PIECE = 128


def tile_moe_shf_mlp_relu2_kernel(
    tc, x_words, x_scales, w1_words, w1_scales, w2_words, w2_scales,
    w1s_words, w1s_scales, w2s_words, w2s_scales, gate, offs, pos1, pos2, out,
):
    nc = tc.nc
    with ExitStack() as ctx:
        keep = ctx.enter_context(tc.tile_pool(name="keep", bufs=1))
        psum = ctx.enter_context(tc.psum_pool(name="psum", bufs=1))

        def held(name, shape, dtype, tag=""):
            return keep.tile(shape, dtype, name=name, tag=tag or name, align_bytes=64)

        def bank(b, shape):
            return psum.tile(shape, F32, name="bank%d" % b)

        offs_t = keep.tile([P, S // 16], U16, name="offs_t")
        pos_t = [keep.tile([P, T // 16], U16, name="pos_t%d" % r) for r in range(2)]
        xw = held("xw", [P, T], I32)
        xs = held("xs", [P, T], U8)
        xgw = [held("xgw%d" % e0, [P, (e1 - e0) * C], U32) for e0, e1 in GATHERS]
        xgs = [held("xgs%d" % e0, [P, (e1 - e0) * C], U8) for e0, e1 in GATHERS]
        w1w = [held("w1w%d" % e0, [P, e1 - e0, 2 * H], U8) for e0, e1 in W1_LOADS]
        w1c = [held("w1c%d" % e0, [P, e1 - e0, H], U8) for e0, e1 in W1_PLANES]
        w2w = [held("w2w%d" % j0, [P, E, 2 * P * (j1 - j0)], U8) for j0, j1 in W2_LOADS]
        w2c = held("w2c", [P, E, N], U8)
        w1sw = held("w1sw", [P, HS], I32)
        w1sc = held("w1sc", [P, 1, HS], U8)
        w2sw = held("w2sw", [P, N], I32)
        w2sc = held("w2sc", [P, 1, N], U8)
        gate_t = held("gate_t", [P, 2, T], F32)
        ident0 = held("ident0", [P, P], F32)
        ident = held("ident", [P, P], F32)
        hb = [held("hb%d" % u0, [P, (u1 - u0) * C, 4], BF16) for u0, u1 in HIDDEN]
        hc = [held("hc%d" % u0, [P, (u1 - u0) * C], U8) for u0, u1 in HIDDEN]
        hw, y = {}, {}

        def place(groups, u):
            g = [u0 <= u < u1 for u0, u1 in groups].index(True)
            return g, u - groups[g][0]

        def load_words(dst, src, queue=nc.sync):
            queue.dma_start(dst[:], src[0].rearrange("p t d -> p (t d)").bitcast(I32))

        def load_token_rows(q, queue):
            rows = x_scales[0, 4 * q : 4 * q + 4, :].bitcast(I32)
            queue.dma_start(xs[32 * q : 32 * (q + 1), :].bitcast(I32), rows.unsqueeze(0).to_broadcast([8, 4, rows.shape[1]]))

        def load_planes(dst, src, queues=(nc.sync,) * 4):
            for r, queue in enumerate(queues):
                queue.dma_start(dst[r:P:32, :, :].bitcast(I32), src[:, r:16:4, :].rearrange("e b i -> b e i").bitcast(I32))

        def load_w2_rows(g):
            j0, j1 = W2_LOADS[g]
            src = w2_words[:, 0, :, 2 * P * j0 : 2 * P * j1].rearrange("e p c -> p e c")
            nc.sync.dma_start(w2w[g][:].bitcast(I32), src.bitcast(I32))

        def load_expert_words(dst, src, e0, e1, queue=nc.sync):
            queue.dma_start(dst[:].bitcast(I32), src[e0:e1, 0].rearrange("e p c -> p e c").bitcast(I32))

        for plane in (w1c[0], w1sc, w1c[1], w2c, w2sc):
            nc.vector.memset(plane[:].rearrange("p e i -> p (e i)").bitcast(I32), 0)
        for q in range(4):
            load_token_rows(q, nc.sync if q < 2 else nc.scalar)
        load_words(xw, x_words)
        nc.sync.dma_start(offs_t[:], offs)
        load_expert_words(w1w[0], w1_words, *W1_LOADS[0])
        load_planes(w1c[0], w1_scales[0:4, 0], (nc.sync,) * 4)
        make_identity(nc, ident0[:])
        load_expert_words(w1w[1], w1_words, *W1_LOADS[1])
        load_planes(w1c[1], w1_scales[4:E, 0])
        load_expert_words(w1w[2], w1_words, *W1_LOADS[2])
        load_expert_words(w1w[3], w1_words, *W1_LOADS[3])
        load_planes(w1sc, w1s_scales, (nc.gpsimd,) * 4)
        load_words(w1sw, w1s_words)
        load_w2_rows(0)
        load_planes(w2c, w2_scales[:, 0])
        for r, pos in enumerate((pos1, pos2)):
            nc.sync.dma_start(pos_t[r][:], pos)
        nc.sync.dma_start(gate_t[:], gate.rearrange("r p t -> p r t"))
        load_w2_rows(1)
        load_planes(w2sc, w2s_scales)
        load_words(w2sw, w2s_words)
        nc.scalar.activation(ident[:], ident0[:], ACT.Relu)

        pre, rect, turned, acc, picked, gated, part, ys, ys_sb, zsum, summed, back, result = ({} for k in range(13))

        def gather_tokens(g):
            e0, e1 = GATHERS[g]
            lst = offs_t[:, e0 * C // 16 : e1 * C // 16]
            nc.vector.tensor_copy(xgw[g][:], xw[:].bitcast(U32).indirect(lst))
            nc.vector.tensor_copy(xgs[g][:], xs[:].indirect(lst))

        def layer1(u, b):
            pre[u] = bank(b, [P, H])
            g, k = place(GATHERS, u)
            w, j = place(W1_LOADS, u)
            c, i = place(W1_PLANES, u)
            cols = slice(C * k, C * (k + 1))
            nc.tensor.matmul_mx(
                out=pre[u][:], lhsT=xgw[g][:, cols].bitcast(FP8X4), lhsT_scale=xgs[g][:, cols],
                rhs=w1w[w][:, j, :].bitcast(FP4X4), rhs_scale=w1c[c][:, i, :], start=True, stop=True,
            )

        def shared1(u, b):
            pre[u] = bank(b, [P, H])
            cols = slice(C * (u - E), C * (u - E + 1))
            nc.tensor.matmul_mx(
                out=pre[u][:], lhsT=xw[:, cols].bitcast(FP8X4), lhsT_scale=xs[:, cols],
                rhs=w1sw[:].bitcast(FP8X4), rhs_scale=w1sc[:, 0, :], start=True, stop=True,
            )

        def rectify(u, tag=""):
            rect[u] = held("rect%d" % u, [P, 4, P], F32, tag)
            src = pre[u][:].rearrange("s (m t) -> s t m", t=4)
            if u in RELU_ON_VECTOR:
                nc.vector.tensor_scalar_max(rect[u][:], src, 0.0)
            else:
                nc.scalar.activation(rect[u][:], src, ACT.Relu)

        def turn(u, b):
            turned[u] = bank(b, [P, 4, P])
            for t in range(4):
                nc.tensor.transpose(turned[u][:, t, :], rect[u][:, t, :], ident[:])

        def square(u):
            g, k = place(HIDDEN, u)
            dst = hb[g][:, C * k : C * (k + 1), :]
            nc.scalar.activation(dst, turned[u][:].rearrange("p t s -> p s t"), ACT.Square)

        def quantise(u0, u1, tag=""):
            g, k = place(HIDDEN, u0)
            if g not in hw:
                hw[g] = held("hw%d" % HIDDEN[g][0], [P, (HIDDEN[g][1] - HIDDEN[g][0]) * C], U32, tag)
            cols = slice(C * k, C * (k + u1 - u0))
            nc.vector.quantize_mx(
                out=hw[g][:, cols].bitcast(FP8X4), scales=hc[g][:, cols], in_=hb[g][:, cols, :].rearrange("p s t -> p (s t)")
            )

        def layer2(j, e0, e1, b):
            acc[j, e0] = bank(b, [P, (e1 - e0) * C])
            for e in range(e0, e1):
                g, k = place(HIDDEN, e)
                w, i = place(W2_LOADS, j)
                cols = slice(C * k, C * (k + 1))
                nc.tensor.matmul_mx(
                    out=acc[j, e0][:, C * (e - e0) : C * (e - e0 + 1)],
                    lhsT=w2w[w][:, e, 2 * P * i : 2 * P * (i + 1)].bitcast(FP4X4), lhsT_scale=w2c[:, e, P * j : P * (j + 1)],
                    rhs=hw[g][:, cols].bitcast(FP8X4), rhs_scale=hc[g][:, cols], start=True, stop=True,
                )

        def layer2_mixed(j, g, b):
            acc[j, g] = bank(b, [P, 2, 2 * C])
            for e in (2 * g, 2 * g + 1, 2 * g + 4, 2 * g + 5):
                h, k = place(HIDDEN, e)
                w, i = place(W2_LOADS, j)
                cols = slice(C * k, C * (k + 1))
                nc.tensor.matmul_mx(
                    out=acc[j, g][:, e // 4, C * (e % 2) : C * (e % 2 + 1)],
                    lhsT=w2w[w][:, e, 2 * P * i : 2 * P * (i + 1)].bitcast(FP4X4), lhsT_scale=w2c[:, e, P * j : P * (j + 1)],
                    rhs=hw[h][:, cols].bitcast(FP8X4), rhs_scale=hc[h][:, cols], start=True, stop=True,
                )

        def drain_mixed(j, g):
            if j not in y:
                y[j] = held("y%d" % j, [P, S], F32)
            nc.scalar.copy(y[j][:].rearrange("p (h g c) -> p g h c", h=2, g=2)[:, g], acc[j, g][:])

        def drain(j, e0, copy=nc.scalar.copy, tag=""):
            if j not in y:
                y[j] = held("y%d" % j, [P, S], F32, tag)
            copy(y[j][:, C * e0 : C * e0 + acc[j, e0].shape[1]], acc[j, e0][:])

        def pick(j, r, t0=0, t1=T, tag=""):
            gated[j, r, t0] = held("picked%d_%d_%d" % (j, r, t0), [P, t1 - t0], F32, tag)
            nc.vector.tensor_tensor(
                gated[j, r, t0][:], y[j][:].indirect(pos_t[r][:, t0 // 16 : t1 // 16]), gate_t[:, r, t0:t1], ALU.mult
            )

        def fetch(j, r, t0=0, t1=T, tag=""):
            picked[j, r, t0] = held("fetched%d_%d_%d" % (j, r, t0), [P, t1 - t0], F32, tag)
            nc.scalar.activation(picked[j, r, t0][:], y[j][:].indirect(pos_t[r][:, t0 // 16 : t1 // 16]), ACT.Copy)

        def weigh(j, r, t0=0, t1=T, base=0, tag=""):
            gated[j, r, t0] = held("gated%d_%d_%d" % (j, r, t0), [P, t1 - t0], F32, tag)
            nc.vector.tensor_tensor(
                gated[j, r, t0][:], picked[j, r, base][:, t0 - base : t1 - base], gate_t[:, r, t0:t1], ALU.mult
            )

        def shared_rows(j, b):
            ys[j] = bank(b, [P, T])
            g = len(HIDDEN) - 1
            nc.tensor.matmul_mx(
                out=ys[j][:], lhsT=w2sw[:, P * j : P * (j + 1)].bitcast(FP8X4), lhsT_scale=w2sc[:, 0, P * j : P * (j + 1)],
                rhs=hw[g][:].bitcast(FP8X4), rhs_scale=hc[g][:], start=True, stop=True,
            )

        def park(j, tag=""):
            ys_sb[j] = held("ys_sb%d" % j, [P, T], F32, tag)
            nc.scalar.copy(ys_sb[j][:], ys[j][:])

        def add_turned(j, term, first=False, last=False):
            for tb in range(4):
                nc.tensor.matmul(
                    zsum[j][:, tb, :], term[:, P * tb : P * (tb + 1)], ident[:],
                    start=(first and tb == 0), stop=(last and tb == 3), is_transpose=True,
                )

        def open_sum(j, b, term):
            zsum[j] = bank(b, [P, 4, P])
            add_turned(j, term, first=True)

        def drain_sum(j, tag="", b0=0, b1=4):
            summed[j, b0] = held("summed%d_%d" % (j, b0), [P, b1 - b0, P], F32, tag)
            nc.scalar.copy(summed[j, b0][:], zsum[j][:, b0:b1, :])

        def turn_back(j, b, b0=0):
            back[j, b0] = bank(b, summed[j, b0].shape)
            for tb in range(summed[j, b0].shape[1]):
                nc.tensor.transpose(back[j, b0][:, tb, :], summed[j, b0][:, tb, :], ident[:])

        def drain_back(j, b0=0):
            result[j, b0] = held("res%d_%d" % (j, b0), back[j, b0].shape, F32)
            nc.scalar.copy(result[j, b0][:], back[j, b0][:])

        def store(j, queue, b0=0):
            rows = result[j, b0][:].rearrange("p a b -> p (a b)")
            queue.dma_start(out[P * j : P * (j + 1), P * b0 : P * b0 + rows.shape[1]], rows)

        def add_shared(j, r, tag=""):
            part[j] = held("part%d" % j, [P, T], F32, tag)
            nc.vector.tensor_tensor(part[j][:], gated[j, r, 0][:], ys[j][:], ALU.add)

        def finish(j, r, t0=0, t1=T, base=None, tag=""):
            base = t0 if base is None else base
            res = held("last%d_%d" % (j, t0), [P, t1 - t0], F32, tag)
            nc.vector.tensor_tensor(res[:], part[j][:, t0:t1], gated[j, r, base][:, t0 - base : t1 - base], ALU.add)
            nc.sync.dma_start(out[P * j : P * (j + 1), t0:t1], res[:])

        for g in range(len(GATHERS)):
            gather_tokens(g)
        for u in range(4):
            layer1(u, u)
        for u in range(4):
            rectify(u)
        turn(0, 4)
        layer1(4, 0)
        layer1(5, 1)
        turn(1, 6)
        turn(2, 7)
        turn(3, 5)
        layer1(6, 2)
        layer1(7, 3)
        rectify(4)
        rectify(5)
        turn(4, 0)
        turn(5, 1)
        for u in range(4):
            square(u)
        rectify(6)
        rectify(7)
        shared1(8, 7)
        turn(6, 6)
        turn(7, 2)
        shared1(9, 3)
        square(4)
        square(5)
        shared1(10, 1)
        shared1(11, 0)
        square(6)
        square(7)
        quantise(0, 4)
        layer2(0, 0, 4, 6)
        rectify(8)
        quantise(4, 6)
        quantise(6, 7)
        rectify(9)
        quantise(7, 8)
        rectify(10)
        rectify(11)
        layer2(0, 4, 7, 2)
        layer2(0, 7, 8, 4)
        drain(0, 0)
        drain(0, 4)
        drain(0, 7, nc.vector.tensor_copy)

        layer2(1, 0, 4, 1)
        layer2(1, 4, 8, 0)
        drain(1, 0)
        drain(1, 4)
        pick(0, 0)
        pick(0, 1)
        pick(1, 0)
        for u, b in zip(range(E, UNITS), (6, 2, 1, 0)):
            turn(u, b)
            square(u)
        quantise(8, 12)
        layer2(2, 0, 4, 6)
        layer2(2, 4, 8, 2)
        layer2(3, 0, 4, 1)
        layer2(3, 4, 8, 0)
        pick(1, 1, tag="hw4")
        for j in (2, 3):
            drain(j, 0)
            drain(j, 4)
        open_sum(0, 6, gated[0, 0, 0])
        add_turned(0, gated[0, 1, 0])
        for j, b in enumerate((4, 5, 7, 3)):
            shared_rows(j, b)
        pick(2, 0)
        pick(2, 1)
        park(0)
        park(1)
        add_turned(0, ys_sb[0], last=True)
        open_sum(1, 2, gated[1, 0, 0])
        add_turned(1, gated[1, 1, 0])
        add_turned(1, ys_sb[1], last=True)
        park(2)
        open_sum(2, 5, gated[2, 0, 0])
        add_turned(2, ys_sb[2])
        drain_sum(0, "summed_a")
        turn_back(0, 1)
        add_turned(2, gated[2, 1, 0], last=True)
        drain_sum(1)
        turn_back(1, 0)
        drain_back(0)
        drain_sum(2, "summed_a", 0, 2)
        store(0, nc.scalar)
        drain_sum(2, "", 2, 4)
        turn_back(2, 4, 0)
        turn_back(2, 7, 2)
        drain_back(1)
        drain_back(2, 0)
        store(1, nc.scalar)
        drain_back(2, 2)
        store(2, nc.scalar, 0)
        store(2, nc.scalar, 2)
        cut = T - LAST_PIECE
        pick(3, 0)
        pick(3, 1, 0, cut)
        add_shared(3, 0)
        pick(3, 1, cut, T)
        finish(3, 1, 0, cut)
        finish(3, 1, cut, T)
